import numpy as np
import ml_dtypes


def mxq(x, axis, fmt="e4m3"):
    dtype, down = {"e4m3": (ml_dtypes.float8_e4m3fn, 7), "e5m2": (ml_dtypes.float8_e5m2, 14)}[fmt]
    v = np.moveaxis(np.asarray(x, np.float32).astype(ml_dtypes.bfloat16).astype(np.float64), axis, -1)
    blocks = v.reshape(v.shape[:-1] + (-1, 32))
    amax = np.abs(blocks).max(-1, keepdims=True)
    byte = np.maximum(np.where(amax > 0, np.frexp(amax)[1] - 1 + 127, 0) - down, 1)
    scale = np.exp2(byte - 127.0)
    codes = (blocks / scale).astype(np.float32).astype(dtype).astype(np.float64)
    return np.moveaxis((codes * scale).reshape(v.shape), -1, axis)


WIDE = False


def mx_kscale(k):
    if not WIDE:
        return np.ones(k)
    levels = np.array([10, -10, 5, -5, 0])
    if k % 512:
        return np.exp2(np.random.permutation(np.resize(levels, k // 32))).repeat(32)
    a = np.empty((k // 512, 16))
    for p in range(k // 512):
        a[p, :8] = np.random.permutation(np.resize(levels, 8))
        for g in range(8):
            far = levels[np.abs(levels - a[p, g]) >= 10]
            a[p, g + 8] = far[np.random.randint(len(far))]
    return np.exp2(a.ravel()).repeat(32)


def f64(x):
    return np.asarray(x).astype(np.float64)


def striped(idx):
    return np.tile(idx.reshape(-1, 16).T, (8, 1)).astype(np.uint16)


def unstriped(offs):
    return offs[:16].T.reshape(-1).astype(np.int64)


E2M1 = np.array([0.0, 0.5, 1.0, 1.5, 2.0, 3.0, 4.0, 6.0, -0.0, -0.5, -1.0, -1.5, -2.0, -3.0, -4.0, -6.0])


def pack_fp4(w):
    k, n = w.shape
    w = f64(np.asarray(w, np.float32).astype(ml_dtypes.bfloat16)).reshape(k // 32, 32, n)
    amax = np.abs(w).max(1)
    mant, ex = np.frexp(amax / 6.0)
    byte = np.clip(np.where(amax > 0, np.where(mant > 0.5, ex, ex - 1) + 127, 1), 1, 254)
    scaled = (w * np.exp2(127.0 - byte)[:, None, :]).reshape(k, n).astype(np.float32)
    c = np.ascontiguousarray(scaled.reshape(k // 512, 128, 4, n).transpose(0, 1, 3, 2)).astype(ml_dtypes.float4_e2m1fn).view(np.uint8) & 0xF
    words = (c[..., 0::2] | (c[..., 1::2] << 4)).reshape(k // 512, 128, 2 * n)
    return np.ascontiguousarray(words), np.ascontiguousarray(byte.astype(np.uint8).reshape(k // 512, 16, n))


def unpack_fp4(words, scales):
    g, _, n = scales.shape
    words = np.ascontiguousarray(words).reshape(g, 128, n, 2)
    nib = np.empty((g, 128, n, 4), np.uint8)
    nib[..., 0::2] = words & 0xF
    nib[..., 1::2] = words >> 4
    vals = E2M1[nib] * np.repeat(np.exp2(scales.astype(np.float64) - 127.0), 8, axis=1)[..., None]
    return vals.transpose(0, 1, 3, 2).reshape(g * 512, n)


def relu(v):
    return np.maximum(v, 0.0)


K, T, S, H, N = 1024, 2048, 512, 512, 128


def setup_inputs():
    n = np.random.standard_normal
    s = mx_kscale(K)[:, None]
    u = mx_kscale(H)
    packed_w1 = pack_fp4(n((K, N)) / np.sqrt(2 * K) / s)
    packed_w3 = pack_fp4(n((H, N)) / np.sqrt(2 * H) / u[:, None])
    return {
        "xT": (n((K, T)) * s).astype(np.float32),
        "w1_words": packed_w1[0],
        "w1_scales": packed_w1[1],
        "w2": (n((K, H)) / np.sqrt(K) / s * u).astype(np.float32),
        "w3_words": packed_w3[0],
        "w3_scales": packed_w3[1],
        "offs": striped(np.random.permutation(T)[:S]),
    }


def reference(xT, w1_words, w1_scales, w2, w3_words, w3_scales, offs):
    xq = mxq(f64(xT)[:, unstriped(offs)], 0, "e4m3")
    h = relu(mxq(f64(w2), 0, "e4m3").T @ xq)
    return unpack_fp4(w1_words, w1_scales).T @ xq + unpack_fp4(w3_words, w3_scales).T @ mxq(h, 0, "e4m3")

@@ -1,0 +1,195 @@
+from contextlib import ExitStack
+
+import concourse.mybir as mybir
+
+K, T, S, H, N = 1024, 2048, 512, 512, 128
+FLOPS = 2 * S * (K * H + K * N + H * N)
+
+F32 = mybir.dt.float32
+BF16 = mybir.dt.bfloat16
+I32 = mybir.dt.int32
+U32 = mybir.dt.uint32
+U16 = mybir.dt.uint16
+U8 = mybir.dt.uint8
+FP8X4 = mybir.dt.float8_e4m3fn_x4
+FP4X4 = mybir.dt.float4_e2m1fn_x4
+RELU = mybir.ActivationFunctionType.Relu
+
+P = 128
+PACK = 4
+K_PASS = P * PACK
+PASSES = K // K_PASS
+G = 128
+GROUPS = S // G
+M_HALF = P // 2
+M_VECTOR = 44
+
+
+def tile_picked_lora_relu_e_kernel(tc, xT, w1_words, w1_scales, w2, w3_words, w3_scales, offs, out):
+    nc = tc.nc
+    with ExitStack() as ctx:
+        keep = ctx.enter_context(tc.tile_pool(name="keep", bufs=1))
+        psum = ctx.enter_context(tc.psum_pool(name="psum", bufs=1))
+
+        offsets = keep.tile([P, S // 16], U16, name="offsets")
+        x_rows = [[keep.tile([P, T], F32, name=f"x_rows{z}{j}") for j in range(PACK)] for z in range(PASSES)]
+        w2_raw = [[keep.tile([P, PACK, H // 2], F32, name=f"w2_raw{z}{u}") for u in range(2)] for z in range(PASSES)]
+        w1_codes = keep.tile([P, PASSES, 2 * N], U8, name="w1_codes", align_bytes=64)
+        w3_codes = keep.tile([P, 2 * N], U8, name="w3_codes", align_bytes=64)
+        w_scales = keep.tile([P, PASSES + 1, N], U8, name="w_scales", align_bytes=64)
+
+        x_view = xT.rearrange("(z p j) t -> z j p t", z=PASSES, j=PACK)
+        w2_view = w2.rearrange("(z p j) (u c) -> z u p j c", z=PASSES, j=PACK, u=2)
+
+        nc.gpsimd.memset(w_scales[:].rearrange("p z c -> p (z c)").bitcast(I32), 0)
+        for q in range(4):
+            nc.gpsimd.dma_start(
+                out=w_scales[32 * q : 32 * q + 4, 0:PASSES, :].bitcast(I32),
+                in_=w1_scales[:, 4 * q : 4 * q + 4, :].rearrange("z r c -> r z c").bitcast(I32),
+            )
+            nc.gpsimd.dma_start(
+                out=w_scales[32 * q : 32 * q + 4, PASSES, :].bitcast(I32),
+                in_=w3_scales[0, 4 * q : 4 * q + 4, :].bitcast(I32),
+            )
+
+        def load_x(z, j):
+            nc.sync.dma_start(out=x_rows[z][j][:], in_=x_view[z, j])
+
+        load_x(0, 0)
+        nc.sync.dma_start(offsets[:], offs)
+        load_x(0, 1)
+        load_x(0, 2)
+        load_x(0, 3)
+        load_x(1, 0)
+        load_x(1, 1)
+        for u in range(2):
+            nc.sync.dma_start(out=w2_raw[0][u][:], in_=w2_view[0, u])
+        load_x(1, 2)
+        load_x(1, 3)
+        for u in range(2):
+            nc.sync.dma_start(out=w2_raw[1][u][:], in_=w2_view[1, u])
+        nc.sync.dma_start(out=w1_codes[:].bitcast(I32), in_=w1_words.rearrange("z p b -> p z b").bitcast(I32))
+        nc.sync.dma_start(out=w3_codes[:].bitcast(I32), in_=w3_words[0].bitcast(I32))
+
+        x_bf = [keep.tile([P, S, PACK], BF16, name=f"x_bf{z}", align_bytes=64) for z in range(PASSES)]
+        x_codes = [keep.tile([P, S], U32, name=f"x_codes{z}", align_bytes=64) for z in range(PASSES)]
+        x_scales = [keep.tile([P, S], U8, name=f"x_scales{z}", align_bytes=64) for z in range(PASSES)]
+        w2_bf = [keep.tile([P, PACK, P, PACK], BF16, name=f"w2_bf{z}", align_bytes=64) for z in range(PASSES)]
+        w2_codes = [keep.tile([P, PACK, P], U32, name=f"w2_codes{z}", align_bytes=64) for z in range(PASSES)]
+        w2_scales = [keep.tile([P, PACK, P], U8, name=f"w2_scales{z}", align_bytes=64) for z in range(PASSES)]
+        h_bank = [psum.tile([P, PACK, G], F32, name=f"h_bank{g}") for g in range(GROUPS)]
+        o_bank = [psum.tile([P, G], F32, name=f"o_bank{g}") for g in range(GROUPS)]
+
+        def gather(z, j):
+            nc.vector.tensor_copy(out=x_bf[z][:, :, j], in_=x_rows[z][j][:].indirect(offsets[:]))
+
+        def quantize_x(z):
+            nc.vector.quantize_mx(out=x_codes[z][:].bitcast(FP8X4), scales=x_scales[z][:], in_=x_bf[z][:].rearrange("p s j -> p (s j)"))
+
+        def w2_copy_views(z, u, m0, m1):
+            dst = w2_bf[z][:].rearrange("p t m j -> p m j t")[:, u * M_HALF + m0 : u * M_HALF + m1]
+            src = w2_raw[z][u][:].rearrange("p j (m t) -> p m j t", t=PACK)[:, m0:m1]
+            return dst, src
+
+        def h_pass(z, g, t, start, stop):
+            cols = slice(g * G, (g + 1) * G)
+            nc.tensor.matmul_mx(
+                out=h_bank[g][:, t, :],
+                lhsT=w2_codes[z][:, t, :].bitcast(FP8X4),
+                lhsT_scale=w2_scales[z][:, t, :],
+                rhs=x_codes[z][:, cols].bitcast(FP8X4),
+                rhs_scale=x_scales[z][:, cols],
+                start=start,
+                stop=stop,
+            )
+
+        for j in range(PACK):
+            gather(0, j)
+        quantize_x(0)
+        gather(1, 0)
+        gather(1, 1)
+        for u in range(2):
+            dst, src = w2_copy_views(0, u, 0, M_HALF)
+            nc.scalar.copy(out=dst, in_=src)
+        gather(1, 2)
+        nc.vector.quantize_mx(
+            out=w2_codes[0][:].rearrange("p t m -> p (t m)").bitcast(FP8X4),
+            scales=w2_scales[0][:].rearrange("p t m -> p (t m)"),
+            in_=w2_bf[0][:].rearrange("p t m j -> p (t m j)"),
+        )
+        for g in range(GROUPS):
+            for t in range(PACK):
+                h_pass(0, g, t, start=(t == 0), stop=False)
+        gather(1, 3)
+        quantize_x(1)
+
+        dst, src = w2_copy_views(1, 0, 0, M_HALF)
+        nc.scalar.copy(out=dst, in_=src)
+        dst, src = w2_copy_views(1, 1, 0, M_VECTOR)
+        nc.vector.tensor_copy(out=dst, in_=src)
+        dst, src = w2_copy_views(1, 1, M_VECTOR, M_HALF)
+        nc.scalar.copy(out=dst, in_=src)
+        for t in range(PACK):
+            nc.vector.quantize_mx(
+                out=w2_codes[1][:, t, :].bitcast(FP8X4),
+                scales=w2_scales[1][:, t, :],
+                in_=w2_bf[1][:, t].rearrange("p m j -> p (m j)"),
+            )
+        for pair in range(GROUPS // 2):
+            for t in range(PACK):
+                for g in (2 * pair, 2 * pair + 1):
+                    h_pass(1, g, t, start=False, stop=(t == PACK - 1))
+
+        for g in range(GROUPS):
+            cols = slice(g * G, (g + 1) * G)
+            for z in (1, 0):
+                nc.tensor.matmul_mx(
+                    out=o_bank[g][:],
+                    lhsT=w1_codes[:, z, :].bitcast(FP4X4),
+                    lhsT_scale=w_scales[:, z, :],
+                    rhs=x_codes[z][:, cols].bitcast(FP8X4),
+                    rhs_scale=x_scales[z][:, cols],
+                    start=(z == 1),
+                    stop=False,
+                )
+
+        h_bf = [keep.tile([P, G, PACK], BF16, name=f"h_bf{g}", align_bytes=64) for g in range(GROUPS)]
+        h_codes = [keep.tile([P, G], U32, name=f"h_codes{g}", align_bytes=64) for g in range(GROUPS)]
+        h_scales = [keep.tile([P, G], U8, name=f"h_scales{g}", align_bytes=64) for g in range(GROUPS)]
+        result = [keep.tile([P, G], F32, name=f"result{g}") for g in range(GROUPS)]
+
+        def relu(g, on_vector, s0, s1):
+            src = h_bank[g][:].rearrange("p t s -> p s t")[:, s0:s1]
+            if on_vector:
+                nc.vector.tensor_scalar_max(out=h_bf[g][:, s0:s1], in0=src, scalar1=0.0)
+            else:
+                nc.scalar.activation(out=h_bf[g][:, s0:s1], in_=src, func=RELU)
+
+        def finish(g):
+            nc.vector.quantize_mx(out=h_codes[g][:].bitcast(FP8X4), scales=h_scales[g][:], in_=h_bf[g][:].rearrange("p s t -> p (s t)"))
+            nc.tensor.matmul_mx(
+                out=o_bank[g][:],
+                lhsT=w3_codes[:].bitcast(FP4X4),
+                lhsT_scale=w_scales[:, PASSES, :],
+                rhs=h_codes[g][:].bitcast(FP8X4),
+                rhs_scale=h_scales[g][:],
+                start=False,
+                stop=True,
+            )
+
+        def store(g):
+            nc.scalar.copy(out=result[g][:], in_=o_bank[g][:])
+            queue = nc.scalar if g == GROUPS - 1 else nc.sync
+            queue.dma_start(out=out[:, g * G : (g + 1) * G], in_=result[g][:])
+
+        relu(0, False, 0, G)
+        relu(1, True, 0, G)
+        relu(2, False, 0, G)
+        finish(0)
+        relu(3, True, 0, G // 2)
+        finish(1)
+        relu(3, False, G // 2, G)
+        finish(2)
+        finish(3)
+        for g in range(GROUPS):
+            store(g)

@@ -22,7 +22,7 @@ PASSES = K // K_PASS
 G = 128
 GROUPS = S // G
 M_HALF = P // 2
-M_VECTOR = 44
+M_VECTOR = 48
 
 
 def tile_picked_lora_relu_e_kernel(tc, xT, w1_words, w1_scales, w2, w3_words, w3_scales, offs, out):
@@ -32,50 +32,48 @@ def tile_picked_lora_relu_e_kernel(tc, xT, w1_words, w1_scales, w2, w3_words, w3
         psum = ctx.enter_context(tc.psum_pool(name="psum", bufs=1))
 
         offsets = keep.tile([P, S // 16], U16, name="offsets")
-        x_rows = [[keep.tile([P, T], F32, name=f"x_rows{z}{j}") for j in range(PACK)] for z in range(PASSES)]
-        w2_raw = [[keep.tile([P, PACK, H // 2], F32, name=f"w2_raw{z}{u}") for u in range(2)] for z in range(PASSES)]
+        x_rows = [[keep.tile([P, T], F32, name=f"x_rows{z}{j}", align_bytes=64) for j in range(PACK)] for z in range(PASSES)]
+        w2_first = keep.tile([P, PACK, H], F32, name="w2_first")
+        w2_last = [keep.tile([P, PACK, H // 2], F32, name=f"w2_last{u}") for u in range(2)]
         w1_codes = keep.tile([P, PASSES, 2 * N], U8, name="w1_codes", align_bytes=64)
         w3_codes = keep.tile([P, 2 * N], U8, name="w3_codes", align_bytes=64)
         w_scales = keep.tile([P, PASSES + 1, N], U8, name="w_scales", align_bytes=64)
 
         x_view = xT.rearrange("(z p j) t -> z j p t", z=PASSES, j=PACK)
-        w2_view = w2.rearrange("(z p j) (u c) -> z u p j c", z=PASSES, j=PACK, u=2)
+        w2_view = w2.rearrange("(z p j) c -> z p j c", z=PASSES, j=PACK)
 
         nc.gpsimd.memset(w_scales[:].rearrange("p z c -> p (z c)").bitcast(I32), 0)
-        for q in range(4):
-            nc.gpsimd.dma_start(
-                out=w_scales[32 * q : 32 * q + 4, 0:PASSES, :].bitcast(I32),
-                in_=w1_scales[:, 4 * q : 4 * q + 4, :].rearrange("z r c -> r z c").bitcast(I32),
-            )
-            nc.gpsimd.dma_start(
-                out=w_scales[32 * q : 32 * q + 4, PASSES, :].bitcast(I32),
-                in_=w3_scales[0, 4 * q : 4 * q + 4, :].bitcast(I32),
-            )
 
         def load_x(z, j):
             nc.sync.dma_start(out=x_rows[z][j][:], in_=x_view[z, j])
 
         load_x(0, 0)
         nc.sync.dma_start(offsets[:], offs)
-        load_x(0, 1)
-        load_x(0, 2)
-        load_x(0, 3)
-        load_x(1, 0)
-        load_x(1, 1)
+        for j in range(1, PACK):
+            load_x(0, j)
+        nc.sync.dma_start(out=w2_first[:], in_=w2_view[0])
+        for j in range(PACK):
+            load_x(1, j)
         for u in range(2):
-            nc.sync.dma_start(out=w2_raw[0][u][:], in_=w2_view[0, u])
-        load_x(1, 2)
-        load_x(1, 3)
-        for u in range(2):
-            nc.sync.dma_start(out=w2_raw[1][u][:], in_=w2_view[1, u])
+            nc.sync.dma_start(out=w2_last[u][:], in_=w2_view[1][:, :, u * (H // 2) : (u + 1) * (H // 2)])
         nc.sync.dma_start(out=w1_codes[:].bitcast(I32), in_=w1_words.rearrange("z p b -> p z b").bitcast(I32))
+        for q in range(4):
+            nc.sync.dma_start(
+                out=w_scales[32 * q : 32 * q + 4, 0:PASSES, :].bitcast(I32),
+                in_=w1_scales[:, 4 * q : 4 * q + 4, :].rearrange("z r c -> r z c").bitcast(I32),
+            )
         nc.sync.dma_start(out=w3_codes[:].bitcast(I32), in_=w3_words[0].bitcast(I32))
+        for q in range(4):
+            nc.sync.dma_start(
+                out=w_scales[32 * q : 32 * q + 4, PASSES, :].bitcast(I32),
+                in_=w3_scales[0, 4 * q : 4 * q + 4, :].bitcast(I32),
+            )
 
         x_bf = [keep.tile([P, S, PACK], BF16, name=f"x_bf{z}", align_bytes=64) for z in range(PASSES)]
         x_codes = [keep.tile([P, S], U32, name=f"x_codes{z}", align_bytes=64) for z in range(PASSES)]
         x_scales = [keep.tile([P, S], U8, name=f"x_scales{z}", align_bytes=64) for z in range(PASSES)]
         w2_bf = [keep.tile([P, PACK, P, PACK], BF16, name=f"w2_bf{z}", align_bytes=64) for z in range(PASSES)]
-        w2_codes = [keep.tile([P, PACK, P], U32, name=f"w2_codes{z}", align_bytes=64) for z in range(PASSES)]
+        w2_codes = {}
         w2_scales = [keep.tile([P, PACK, P], U8, name=f"w2_scales{z}", align_bytes=64) for z in range(PASSES)]
         h_bank = [psum.tile([P, PACK, G], F32, name=f"h_bank{g}") for g in range(GROUPS)]
         o_bank = [psum.tile([P, G], F32, name=f"o_bank{g}") for g in range(GROUPS)]
@@ -86,16 +84,24 @@ def tile_picked_lora_relu_e_kernel(tc, xT, w1_words, w1_scales, w2, w3_words, w3
         def quantize_x(z):
             nc.vector.quantize_mx(out=x_codes[z][:].bitcast(FP8X4), scales=x_scales[z][:], in_=x_bf[z][:].rearrange("p s j -> p (s j)"))
 
-        def w2_copy_views(z, u, m0, m1):
-            dst = w2_bf[z][:].rearrange("p t m j -> p m j t")[:, u * M_HALF + m0 : u * M_HALF + m1]
-            src = w2_raw[z][u][:].rearrange("p j (m t) -> p m j t", t=PACK)[:, m0:m1]
+        def w2_copy_views(z, raw, first, m0, m1):
+            dst = w2_bf[z][:].rearrange("p t m j -> p m t j")[:, first + m0 : first + m1]
+            src = raw[:].rearrange("p j (m t) -> p m t j", t=PACK)[:, m0:m1]
             return dst, src
+
+        def quantize_w2(z, t, tag):
+            w2_codes[z, t] = keep.tile([P, P], U32, name=f"w2_codes{z}{t}", tag=tag, align_bytes=64)
+            nc.vector.quantize_mx(
+                out=w2_codes[z, t][:].bitcast(FP8X4),
+                scales=w2_scales[z][:, t, :],
+                in_=w2_bf[z][:, t].rearrange("p m j -> p (m j)"),
+            )
 
         def h_pass(z, g, t, start, stop):
             cols = slice(g * G, (g + 1) * G)
             nc.tensor.matmul_mx(
                 out=h_bank[g][:, t, :],
-                lhsT=w2_codes[z][:, t, :].bitcast(FP8X4),
+                lhsT=w2_codes[z, t][:].bitcast(FP8X4),
                 lhsT_scale=w2_scales[z][:, t, :],
                 rhs=x_codes[z][:, cols].bitcast(FP8X4),
                 rhs_scale=x_scales[z][:, cols],
@@ -106,35 +112,28 @@ def tile_picked_lora_relu_e_kernel(tc, xT, w1_words, w1_scales, w2, w3_words, w3
         for j in range(PACK):
             gather(0, j)
         quantize_x(0)
+        dst, src = w2_copy_views(0, w2_first, 0, 0, P)
+        nc.scalar.copy(out=dst, in_=src)
         gather(1, 0)
+        for t in range(1, PACK):
+            quantize_w2(0, t, f"w2_codes0{t}")
         gather(1, 1)
-        for u in range(2):
-            dst, src = w2_copy_views(0, u, 0, M_HALF)
-            nc.scalar.copy(out=dst, in_=src)
         gather(1, 2)
-        nc.vector.quantize_mx(
-            out=w2_codes[0][:].rearrange("p t m -> p (t m)").bitcast(FP8X4),
-            scales=w2_scales[0][:].rearrange("p t m -> p (t m)"),
-            in_=w2_bf[0][:].rearrange("p t m j -> p (t m j)"),
-        )
+        quantize_w2(0, 0, "x_rows12")
         for g in range(GROUPS):
             for t in range(PACK):
                 h_pass(0, g, t, start=(t == 0), stop=False)
         gather(1, 3)
         quantize_x(1)
 
-        dst, src = w2_copy_views(1, 0, 0, M_HALF)
+        dst, src = w2_copy_views(1, w2_last[0], 0, 0, M_HALF)
         nc.scalar.copy(out=dst, in_=src)
-        dst, src = w2_copy_views(1, 1, 0, M_VECTOR)
+        dst, src = w2_copy_views(1, w2_last[1], M_HALF, 0, M_VECTOR)
         nc.vector.tensor_copy(out=dst, in_=src)
-        dst, src = w2_copy_views(1, 1, M_VECTOR, M_HALF)
+        dst, src = w2_copy_views(1, w2_last[1], M_HALF, M_VECTOR, M_HALF)
         nc.scalar.copy(out=dst, in_=src)
         for t in range(PACK):
-            nc.vector.quantize_mx(
-                out=w2_codes[1][:, t, :].bitcast(FP8X4),
-                scales=w2_scales[1][:, t, :],
-                in_=w2_bf[1][:, t].rearrange("p m j -> p (m j)"),
-            )
+            quantize_w2(1, t, f"w2_codes1{t}")
         for pair in range(GROUPS // 2):
             for t in range(PACK):
                 for g in (2 * pair, 2 * pair + 1):

@@ -21,8 +21,7 @@ K_PASS = P * PACK
 PASSES = K // K_PASS
 G = 128
 GROUPS = S // G
-M_HALF = P // 2
-M_VECTOR = 48
+M_VECTOR = 84
 
 
 def tile_picked_lora_relu_e_kernel(tc, xT, w1_words, w1_scales, w2, w3_words, w3_scales, offs, out):
@@ -32,36 +31,33 @@ def tile_picked_lora_relu_e_kernel(tc, xT, w1_words, w1_scales, w2, w3_words, w3
         psum = ctx.enter_context(tc.psum_pool(name="psum", bufs=1))
 
         offsets = keep.tile([P, S // 16], U16, name="offsets")
-        x_rows = [[keep.tile([P, T], F32, name=f"x_rows{z}{j}", align_bytes=64) for j in range(PACK)] for z in range(PASSES)]
-        w2_first = keep.tile([P, PACK, H], F32, name="w2_first")
-        w2_last = [keep.tile([P, PACK, H // 2], F32, name=f"w2_last{u}") for u in range(2)]
+        x_pairs = [keep.tile([P, 2, T], F32, name=f"x_pair{u}", align_bytes=64) for u in range(2)]
+        x_rows = [keep.tile([P, T], F32, name=f"x_rows{j}", align_bytes=64) for j in range(PACK)]
+        windows = [[x_pairs[j // 2][:, j % 2, :] for j in range(PACK)], [x_rows[j][:] for j in range(PACK)]]
+        w2_raw = [keep.tile([P, PACK, H], F32, name=f"w2_raw{z}") for z in range(PASSES)]
         w1_codes = keep.tile([P, PASSES, 2 * N], U8, name="w1_codes", align_bytes=64)
         w3_codes = keep.tile([P, 2 * N], U8, name="w3_codes", align_bytes=64)
         w_scales = keep.tile([P, PASSES + 1, N], U8, name="w_scales", align_bytes=64)
 
-        x_view = xT.rearrange("(z p j) t -> z j p t", z=PASSES, j=PACK)
+        x_view = xT.rearrange("(z p j) t -> z p j t", z=PASSES, j=PACK)
         w2_view = w2.rearrange("(z p j) c -> z p j c", z=PASSES, j=PACK)
 
         nc.gpsimd.memset(w_scales[:].rearrange("p z c -> p (z c)").bitcast(I32), 0)
 
-        def load_x(z, j):
-            nc.sync.dma_start(out=x_rows[z][j][:], in_=x_view[z, j])
-
-        load_x(0, 0)
-        nc.sync.dma_start(offsets[:], offs)
-        for j in range(1, PACK):
-            load_x(0, j)
-        nc.sync.dma_start(out=w2_first[:], in_=w2_view[0])
-        for j in range(PACK):
-            load_x(1, j)
-        for u in range(2):
-            nc.sync.dma_start(out=w2_last[u][:], in_=w2_view[1][:, :, u * (H // 2) : (u + 1) * (H // 2)])
-        nc.sync.dma_start(out=w1_codes[:].bitcast(I32), in_=w1_words.rearrange("z p b -> p z b").bitcast(I32))
         for q in range(4):
-            nc.sync.dma_start(
+            nc.gpsimd.dma_start(
                 out=w_scales[32 * q : 32 * q + 4, 0:PASSES, :].bitcast(I32),
                 in_=w1_scales[:, 4 * q : 4 * q + 4, :].rearrange("z r c -> r z c").bitcast(I32),
             )
+
+        nc.sync.dma_start(out=x_pairs[0][:], in_=x_view[0][:, 0:2, :])
+        nc.sync.dma_start(offsets[:], offs)
+        nc.sync.dma_start(out=x_pairs[1][:], in_=x_view[0][:, 2:4, :])
+        nc.sync.dma_start(out=w2_raw[0][:], in_=w2_view[0])
+        for j in range(PACK):
+            nc.sync.dma_start(out=x_rows[j][:], in_=x_view[1][:, j, :])
+        nc.sync.dma_start(out=w1_codes[:].bitcast(I32), in_=w1_words.rearrange("z p b -> p z b").bitcast(I32))
+        nc.sync.dma_start(out=w2_raw[1][:], in_=w2_view[1])
         nc.sync.dma_start(out=w3_codes[:].bitcast(I32), in_=w3_words[0].bitcast(I32))
         for q in range(4):
             nc.sync.dma_start(
@@ -78,15 +74,19 @@ def tile_picked_lora_relu_e_kernel(tc, xT, w1_words, w1_scales, w2, w3_words, w3
         h_bank = [psum.tile([P, PACK, G], F32, name=f"h_bank{g}") for g in range(GROUPS)]
         o_bank = [psum.tile([P, G], F32, name=f"o_bank{g}") for g in range(GROUPS)]
 
-        def gather(z, j):
-            nc.vector.tensor_copy(out=x_bf[z][:, :, j], in_=x_rows[z][j][:].indirect(offsets[:]))
+        def gather(z, j, s0, s1):
+            nc.vector.tensor_copy(out=x_bf[z][:, s0:s1, j], in_=windows[z][j].indirect(offsets[:, s0 // 16 : s1 // 16]))
 
-        def quantize_x(z):
-            nc.vector.quantize_mx(out=x_codes[z][:].bitcast(FP8X4), scales=x_scales[z][:], in_=x_bf[z][:].rearrange("p s j -> p (s j)"))
+        def quantize_x(z, s0, s1):
+            nc.vector.quantize_mx(
+                out=x_codes[z][:, s0:s1].bitcast(FP8X4),
+                scales=x_scales[z][:, s0:s1],
+                in_=x_bf[z][:, s0:s1].rearrange("p s j -> p (s j)"),
+            )
 
-        def w2_copy_views(z, raw, first, m0, m1):
-            dst = w2_bf[z][:].rearrange("p t m j -> p m t j")[:, first + m0 : first + m1]
-            src = raw[:].rearrange("p j (m t) -> p m t j", t=PACK)[:, m0:m1]
+        def w2_copy_views(z, m0, m1, t0, t1):
+            dst = w2_bf[z][:].rearrange("p t m j -> p m t j")[:, m0:m1, t0:t1]
+            src = w2_raw[z][:].rearrange("p j (m t) -> p m t j", t=PACK)[:, m0:m1, t0:t1]
             return dst, src
 
         def quantize_w2(z, t, tag):
@@ -110,35 +110,23 @@ def tile_picked_lora_relu_e_kernel(tc, xT, w1_words, w1_scales, w2, w3_words, w3
             )
 
         for j in range(PACK):
-            gather(0, j)
-        quantize_x(0)
-        dst, src = w2_copy_views(0, w2_first, 0, 0, P)
+            gather(0, j, 0, S)
+        quantize_x(0, 0, S)
+        dst, src = w2_copy_views(0, 0, P, 0, PACK)
         nc.scalar.copy(out=dst, in_=src)
-        gather(1, 0)
+        gather(1, 0, 0, S)
         for t in range(1, PACK):
             quantize_w2(0, t, f"w2_codes0{t}")
-        gather(1, 1)
-        gather(1, 2)
-        quantize_w2(0, 0, "x_rows12")
+        gather(1, 1, 0, S)
+        gather(1, 2, 0, S)
+        quantize_w2(0, 0, "x_rows2")
         for g in range(GROUPS):
             for t in range(PACK):
                 h_pass(0, g, t, start=(t == 0), stop=False)
-        gather(1, 3)
-        quantize_x(1)
-
-        dst, src = w2_copy_views(1, w2_last[0], 0, 0, M_HALF)
-        nc.scalar.copy(out=dst, in_=src)
-        dst, src = w2_copy_views(1, w2_last[1], M_HALF, 0, M_VECTOR)
-        nc.vector.tensor_copy(out=dst, in_=src)
-        dst, src = w2_copy_views(1, w2_last[1], M_HALF, M_VECTOR, M_HALF)
-        nc.scalar.copy(out=dst, in_=src)
-        for t in range(PACK):
-            quantize_w2(1, t, f"w2_codes1{t}")
-        for pair in range(GROUPS // 2):
-            for t in range(PACK):
-                for g in (2 * pair, 2 * pair + 1):
-                    h_pass(1, g, t, start=False, stop=(t == PACK - 1))
-
+        gather(1, 3, 0, S // 2)
+        gather(1, 3, S // 2, S)
+        quantize_x(1, 0, S // 2)
+        quantize_x(1, S // 2, S)
         for g in range(GROUPS):
             cols = slice(g * G, (g + 1) * G)
             for z in (1, 0):
@@ -151,6 +139,18 @@ def tile_picked_lora_relu_e_kernel(tc, xT, w1_words, w1_scales, w2, w3_words, w3
                     start=(z == 1),
                     stop=False,
                 )
+
+        for t0 in (0, 2):
+            dst, src = w2_copy_views(1, 0, M_VECTOR, t0, t0 + 2)
+            nc.vector.tensor_copy(out=dst, in_=src)
+            dst, src = w2_copy_views(1, M_VECTOR, P, t0, t0 + 2)
+            nc.scalar.copy(out=dst, in_=src)
+        for t in range(PACK):
+            quantize_w2(1, t, f"w2_codes1{t}")
+        for pair in range(GROUPS // 2):
+            for t in range(PACK):
+                for g in (2 * pair, 2 * pair + 1):
+                    h_pass(1, g, t, start=False, stop=(t == PACK - 1))
 
         h_bf = [keep.tile([P, G, PACK], BF16, name=f"h_bf{g}", align_bytes=64) for g in range(GROUPS)]
         h_codes = [keep.tile([P, G], U32, name=f"h_codes{g}", align_bytes=64) for g in range(GROUPS)]

@@ -21,7 +21,7 @@ K_PASS = P * PACK
 PASSES = K // K_PASS
 G = 128
 GROUPS = S // G
-M_VECTOR = 84
+M_VECTOR = 72
 
 
 def tile_picked_lora_relu_e_kernel(tc, xT, w1_words, w1_scales, w2, w3_words, w3_scales, offs, out):
@@ -44,20 +44,19 @@ def tile_picked_lora_relu_e_kernel(tc, xT, w1_words, w1_scales, w2, w3_words, w3
 
         nc.gpsimd.memset(w_scales[:].rearrange("p z c -> p (z c)").bitcast(I32), 0)
 
-        for q in range(4):
-            nc.gpsimd.dma_start(
-                out=w_scales[32 * q : 32 * q + 4, 0:PASSES, :].bitcast(I32),
-                in_=w1_scales[:, 4 * q : 4 * q + 4, :].rearrange("z r c -> r z c").bitcast(I32),
-            )
-
         nc.sync.dma_start(out=x_pairs[0][:], in_=x_view[0][:, 0:2, :])
         nc.sync.dma_start(offsets[:], offs)
         nc.sync.dma_start(out=x_pairs[1][:], in_=x_view[0][:, 2:4, :])
         nc.sync.dma_start(out=w2_raw[0][:], in_=w2_view[0])
         for j in range(PACK):
             nc.sync.dma_start(out=x_rows[j][:], in_=x_view[1][:, j, :])
-        nc.sync.dma_start(out=w1_codes[:].bitcast(I32), in_=w1_words.rearrange("z p b -> p z b").bitcast(I32))
         nc.sync.dma_start(out=w2_raw[1][:], in_=w2_view[1])
+        nc.sync.dma_start(out=w1_codes[:].bitcast(I32), in_=w1_words.rearrange("z p b -> p z b").bitcast(I32))
+        for q in range(4):
+            nc.sync.dma_start(
+                out=w_scales[32 * q : 32 * q + 4, 0:PASSES, :].bitcast(I32),
+                in_=w1_scales[:, 4 * q : 4 * q + 4, :].rearrange("z r c -> r z c").bitcast(I32),
+            )
         nc.sync.dma_start(out=w3_codes[:].bitcast(I32), in_=w3_words[0].bitcast(I32))
         for q in range(4):
             nc.sync.dma_start(

@@ -51,12 +51,12 @@ def tile_picked_lora_relu_e_kernel(tc, xT, w1_words, w1_scales, w2, w3_words, w3
         for j in range(PACK):
             nc.sync.dma_start(out=x_rows[j][:], in_=x_view[1][:, j, :])
         nc.sync.dma_start(out=w2_raw[1][:], in_=w2_view[1])
-        nc.sync.dma_start(out=w1_codes[:].bitcast(I32), in_=w1_words.rearrange("z p b -> p z b").bitcast(I32))
         for q in range(4):
             nc.sync.dma_start(
                 out=w_scales[32 * q : 32 * q + 4, 0:PASSES, :].bitcast(I32),
                 in_=w1_scales[:, 4 * q : 4 * q + 4, :].rearrange("z r c -> r z c").bitcast(I32),
             )
+        nc.sync.dma_start(out=w1_codes[:].bitcast(I32), in_=w1_words.rearrange("z p b -> p z b").bitcast(I32))
         nc.sync.dma_start(out=w3_codes[:].bitcast(I32), in_=w3_words[0].bitcast(I32))
         for q in range(4):
             nc.sync.dma_start(
@@ -67,11 +67,12 @@ def tile_picked_lora_relu_e_kernel(tc, xT, w1_words, w1_scales, w2, w3_words, w3
         x_bf = [keep.tile([P, S, PACK], BF16, name=f"x_bf{z}", align_bytes=64) for z in range(PASSES)]
         x_codes = [keep.tile([P, S], U32, name=f"x_codes{z}", align_bytes=64) for z in range(PASSES)]
         x_scales = [keep.tile([P, S], U8, name=f"x_scales{z}", align_bytes=64) for z in range(PASSES)]
-        w2_bf = [keep.tile([P, PACK, P, PACK], BF16, name=f"w2_bf{z}", align_bytes=64) for z in range(PASSES)]
+        w2_bf = [keep.tile([P, PACK, P, PACK], BF16, name=f"w2_bf{z}", tag=f"w2_bf{z}", align_bytes=64) for z in range(PASSES)]
         w2_codes = {}
         w2_scales = [keep.tile([P, PACK, P], U8, name=f"w2_scales{z}", align_bytes=64) for z in range(PASSES)]
-        h_bank = [psum.tile([P, PACK, G], F32, name=f"h_bank{g}") for g in range(GROUPS)]
-        o_bank = [psum.tile([P, G], F32, name=f"o_bank{g}") for g in range(GROUPS)]
+        h_bank = [psum.tile([P, PACK, G], F32, name=f"h_bank{g}", tag=f"bank{g}") for g in range(GROUPS)]
+        o_tile = [psum.tile([P, S], F32, name=f"o_bank{g}") for g in range(GROUPS)]
+        o_bank = [o_tile[g][:, 0:G] for g in range(GROUPS)]
 
         def gather(z, j, s0, s1):
             nc.vector.tensor_copy(out=x_bf[z][:, s0:s1, j], in_=windows[z][j].indirect(offsets[:, s0 // 16 : s1 // 16]))
@@ -124,20 +125,23 @@ def tile_picked_lora_relu_e_kernel(tc, xT, w1_words, w1_scales, w2, w3_words, w3
                 h_pass(0, g, t, start=(t == 0), stop=False)
         gather(1, 3, 0, S // 2)
         gather(1, 3, S // 2, S)
+
+        def warm_up(s1):
+            nc.tensor.matmul_mx(
+                out=o_tile[GROUPS - 1][:, 0:s1],
+                lhsT=w2_codes[0, 1][:].bitcast(FP8X4),
+                lhsT_scale=w2_scales[0][:, 1, :],
+                rhs=x_codes[1][:, 0:s1].bitcast(FP8X4),
+                rhs_scale=x_scales[1][:, 0:s1],
+                start=True,
+                stop=True,
+            )
+
         quantize_x(1, 0, S // 2)
+        warm_up(S // 2)
+        warm_up(S // 2)
         quantize_x(1, S // 2, S)
-        for g in range(GROUPS):
-            cols = slice(g * G, (g + 1) * G)
-            for z in (1, 0):
-                nc.tensor.matmul_mx(
-                    out=o_bank[g][:],
-                    lhsT=w1_codes[:, z, :].bitcast(FP4X4),
-                    lhsT_scale=w_scales[:, z, :],
-                    rhs=x_codes[z][:, cols].bitcast(FP8X4),
-                    rhs_scale=x_scales[z][:, cols],
-                    start=(z == 1),
-                    stop=False,
-                )
+        warm_up(S)
 
         for t0 in (0, 2):
             dst, src = w2_copy_views(1, 0, M_VECTOR, t0, t0 + 2)
@@ -163,10 +167,29 @@ def tile_picked_lora_relu_e_kernel(tc, xT, w1_words, w1_scales, w2, w3_words, w3
             else:
                 nc.scalar.activation(out=h_bf[g][:, s0:s1], in_=src, func=RELU)
 
+        w1_plane = keep.tile([P, PASSES, N], U8, name="w1_plane", tag="w2_bf1", align_bytes=64)
+        nc.gpsimd.tensor_copy(
+            out=w1_plane[:].rearrange("p z c -> p (z c)").bitcast(I32),
+            in_=w_scales[:, 0:PASSES, :].rearrange("p z c -> p (z c)").bitcast(I32),
+        )
+
+        def w1_passes(g):
+            cols = slice(g * G, (g + 1) * G)
+            for z in range(PASSES):
+                nc.tensor.matmul_mx(
+                    out=o_bank[g],
+                    lhsT=w1_codes[:, z, :].bitcast(FP4X4),
+                    lhsT_scale=w1_plane[:, z, :],
+                    rhs=x_codes[z][:, cols].bitcast(FP8X4),
+                    rhs_scale=x_scales[z][:, cols],
+                    start=(z == 0),
+                    stop=False,
+                )
+
         def finish(g):
             nc.vector.quantize_mx(out=h_codes[g][:].bitcast(FP8X4), scales=h_scales[g][:], in_=h_bf[g][:].rearrange("p s t -> p (s t)"))
             nc.tensor.matmul_mx(
-                out=o_bank[g][:],
+                out=o_bank[g],
                 lhsT=w3_codes[:].bitcast(FP4X4),
                 lhsT_scale=w_scales[:, PASSES, :],
                 rhs=h_codes[g][:].bitcast(FP8X4),
@@ -176,10 +199,12 @@ def tile_picked_lora_relu_e_kernel(tc, xT, w1_words, w1_scales, w2, w3_words, w3
             )
 
         def store(g):
-            nc.scalar.copy(out=result[g][:], in_=o_bank[g][:])
+            nc.scalar.copy(out=result[g][:], in_=o_bank[g])
             queue = nc.scalar if g == GROUPS - 1 else nc.sync
             queue.dma_start(out=out[:, g * G : (g + 1) * G], in_=result[g][:])
 
+        for g in range(GROUPS):
+            w1_passes(g)
         relu(0, False, 0, G)
         relu(1, True, 0, G)
         relu(2, False, 0, G)

@@ -21,7 +21,7 @@ K_PASS = P * PACK
 PASSES = K // K_PASS
 G = 128
 GROUPS = S // G
-M_VECTOR = 72
+M_VECTOR = 74
 
 
 def tile_picked_lora_relu_e_kernel(tc, xT, w1_words, w1_scales, w2, w3_words, w3_scales, offs, out):
@@ -34,7 +34,7 @@ def tile_picked_lora_relu_e_kernel(tc, xT, w1_words, w1_scales, w2, w3_words, w3
         x_pairs = [keep.tile([P, 2, T], F32, name=f"x_pair{u}", align_bytes=64) for u in range(2)]
         x_rows = [keep.tile([P, T], F32, name=f"x_rows{j}", align_bytes=64) for j in range(PACK)]
         windows = [[x_pairs[j // 2][:, j % 2, :] for j in range(PACK)], [x_rows[j][:] for j in range(PACK)]]
-        w2_raw = [keep.tile([P, PACK, H], F32, name=f"w2_raw{z}") for z in range(PASSES)]
+        w2_raw = [keep.tile([P, PACK, H], F32, name=f"w2_raw{z}", tag=f"w2_raw{z}", align_bytes=64) for z in range(PASSES)]
         w1_codes = keep.tile([P, PASSES, 2 * N], U8, name="w1_codes", align_bytes=64)
         w3_codes = keep.tile([P, 2 * N], U8, name="w3_codes", align_bytes=64)
         w_scales = keep.tile([P, PASSES + 1, N], U8, name="w_scales", align_bytes=64)
@@ -64,8 +64,8 @@ def tile_picked_lora_relu_e_kernel(tc, xT, w1_words, w1_scales, w2, w3_words, w3
                 in_=w3_scales[0, 4 * q : 4 * q + 4, :].bitcast(I32),
             )
 
-        x_bf = [keep.tile([P, S, PACK], BF16, name=f"x_bf{z}", align_bytes=64) for z in range(PASSES)]
-        x_codes = [keep.tile([P, S], U32, name=f"x_codes{z}", align_bytes=64) for z in range(PASSES)]
+        x_bf = [keep.tile([P, S, PACK], BF16, name=f"x_bf{z}", tag=f"x_bf{z}", align_bytes=64) for z in range(PASSES)]
+        x_codes = {}
         x_scales = [keep.tile([P, S], U8, name=f"x_scales{z}", align_bytes=64) for z in range(PASSES)]
         w2_bf = [keep.tile([P, PACK, P, PACK], BF16, name=f"w2_bf{z}", tag=f"w2_bf{z}", align_bytes=64) for z in range(PASSES)]
         w2_codes = {}
@@ -77,16 +77,21 @@ def tile_picked_lora_relu_e_kernel(tc, xT, w1_words, w1_scales, w2, w3_words, w3
         def gather(z, j, s0, s1):
             nc.vector.tensor_copy(out=x_bf[z][:, s0:s1, j], in_=windows[z][j].indirect(offsets[:, s0 // 16 : s1 // 16]))
 
-        def quantize_x(z, s0, s1):
-            nc.vector.quantize_mx(
-                out=x_codes[z][:, s0:s1].bitcast(FP8X4),
-                scales=x_scales[z][:, s0:s1],
-                in_=x_bf[z][:, s0:s1].rearrange("p s j -> p (s j)"),
-            )
+        def quantize_x(z, s0, s1, tag, step):
+            codes = keep.tile([P, s1 - s0], U32, name=f"x_codes{z}_{s0}", tag=tag, align_bytes=64)
+            for g in range(s0 // G, s1 // G):
+                x_codes[z, g] = codes[:, g * G - s0 : (g + 1) * G - s0]
+            x_codes[z, "all", s0] = codes[:]
+            for a in range(s0, s1, step):
+                nc.vector.quantize_mx(
+                    out=codes[:, a - s0 : a - s0 + step].bitcast(FP8X4),
+                    scales=x_scales[z][:, a : a + step],
+                    in_=x_bf[z][:, a : a + step].rearrange("p s j -> p (s j)"),
+                )
 
         def w2_copy_views(z, m0, m1, t0, t1):
-            dst = w2_bf[z][:].rearrange("p t m j -> p m t j")[:, m0:m1, t0:t1]
-            src = w2_raw[z][:].rearrange("p j (m t) -> p m t j", t=PACK)[:, m0:m1, t0:t1]
+            dst = w2_bf[z][:].rearrange("p t m j -> p m j t")[:, m0:m1, :, t0:t1]
+            src = w2_raw[z][:].rearrange("p j (m t) -> p m j t", t=PACK)[:, m0:m1, :, t0:t1]
             return dst, src
 
         def quantize_w2(z, t, tag):
@@ -103,7 +108,7 @@ def tile_picked_lora_relu_e_kernel(tc, xT, w1_words, w1_scales, w2, w3_words, w3
                 out=h_bank[g][:, t, :],
                 lhsT=w2_codes[z, t][:].bitcast(FP8X4),
                 lhsT_scale=w2_scales[z][:, t, :],
-                rhs=x_codes[z][:, cols].bitcast(FP8X4),
+                rhs=x_codes[z, g].bitcast(FP8X4),
                 rhs_scale=x_scales[z][:, cols],
                 start=start,
                 stop=stop,
@@ -111,7 +116,7 @@ def tile_picked_lora_relu_e_kernel(tc, xT, w1_words, w1_scales, w2, w3_words, w3
 
         for j in range(PACK):
             gather(0, j, 0, S)
-        quantize_x(0, 0, S)
+        quantize_x(0, 0, S, "x_codes0", S)
         dst, src = w2_copy_views(0, 0, P, 0, PACK)
         nc.scalar.copy(out=dst, in_=src)
         gather(1, 0, 0, S)
@@ -131,17 +136,15 @@ def tile_picked_lora_relu_e_kernel(tc, xT, w1_words, w1_scales, w2, w3_words, w3
                 out=o_tile[GROUPS - 1][:, 0:s1],
                 lhsT=w2_codes[0, 1][:].bitcast(FP8X4),
                 lhsT_scale=w2_scales[0][:, 1, :],
-                rhs=x_codes[1][:, 0:s1].bitcast(FP8X4),
+                rhs=x_codes[1, "all", 0].bitcast(FP8X4),
                 rhs_scale=x_scales[1][:, 0:s1],
                 start=True,
                 stop=True,
             )
 
-        quantize_x(1, 0, S // 2)
-        warm_up(S // 2)
-        warm_up(S // 2)
-        quantize_x(1, S // 2, S)
-        warm_up(S)
+        quantize_x(1, 0, S // 2, "x_codes1", S // 2)
+        for repeat in range(4):
+            warm_up(S // 2)
 
         for t0 in (0, 2):
             dst, src = w2_copy_views(1, 0, M_VECTOR, t0, t0 + 2)
@@ -150,6 +153,7 @@ def tile_picked_lora_relu_e_kernel(tc, xT, w1_words, w1_scales, w2, w3_words, w3
             nc.scalar.copy(out=dst, in_=src)
         for t in range(PACK):
             quantize_w2(1, t, f"w2_codes1{t}")
+        quantize_x(1, S // 2, S, "w2_raw1", G)
         for pair in range(GROUPS // 2):
             for t in range(PACK):
                 for g in (2 * pair, 2 * pair + 1):
@@ -167,7 +171,7 @@ def tile_picked_lora_relu_e_kernel(tc, xT, w1_words, w1_scales, w2, w3_words, w3
             else:
                 nc.scalar.activation(out=h_bf[g][:, s0:s1], in_=src, func=RELU)
 
-        w1_plane = keep.tile([P, PASSES, N], U8, name="w1_plane", tag="w2_bf1", align_bytes=64)
+        w1_plane = keep.tile([P, PASSES, N], U8, name="w1_plane", tag="x_bf1", align_bytes=64)
         nc.gpsimd.tensor_copy(
             out=w1_plane[:].rearrange("p z c -> p (z c)").bitcast(I32),
             in_=w_scales[:, 0:PASSES, :].rearrange("p z c -> p (z c)").bitcast(I32),
@@ -180,7 +184,7 @@ def tile_picked_lora_relu_e_kernel(tc, xT, w1_words, w1_scales, w2, w3_words, w3
                     out=o_bank[g],
                     lhsT=w1_codes[:, z, :].bitcast(FP4X4),
                     lhsT_scale=w1_plane[:, z, :],
-                    rhs=x_codes[z][:, cols].bitcast(FP8X4),
+                    rhs=x_codes[z, g].bitcast(FP8X4),
                     rhs_scale=x_scales[z][:, cols],
                     start=(z == 0),
                     stop=False,

@@ -21,7 +21,10 @@ K_PASS = P * PACK
 PASSES = K // K_PASS
 G = 128
 GROUPS = S // G
-M_VECTOR = 74
+M_WHOLE = 74
+M_EARLY = 48
+S_VECTOR = 80
+M_LATE = 72
 
 
 def tile_picked_lora_relu_e_kernel(tc, xT, w1_words, w1_scales, w2, w3_words, w3_scales, offs, out):
@@ -31,10 +34,11 @@ def tile_picked_lora_relu_e_kernel(tc, xT, w1_words, w1_scales, w2, w3_words, w3
         psum = ctx.enter_context(tc.psum_pool(name="psum", bufs=1))
 
         offsets = keep.tile([P, S // 16], U16, name="offsets")
-        x_pairs = [keep.tile([P, 2, T], F32, name=f"x_pair{u}", align_bytes=64) for u in range(2)]
-        x_rows = [keep.tile([P, T], F32, name=f"x_rows{j}", align_bytes=64) for j in range(PACK)]
-        windows = [[x_pairs[j // 2][:, j % 2, :] for j in range(PACK)], [x_rows[j][:] for j in range(PACK)]]
-        w2_raw = [keep.tile([P, PACK, H], F32, name=f"w2_raw{z}", tag=f"w2_raw{z}", align_bytes=64) for z in range(PASSES)]
+        x_pairs = [keep.tile([P, 2, T], F32, name=f"x_pair{u}", align_bytes=64) for u in range(3)]
+        x_rows = [keep.tile([P, T], F32, name=f"x_rows{j}", align_bytes=64) for j in range(2)]
+        windows = [[x_pairs[j // 2][:, j % 2, :] for j in range(PACK)], [x_pairs[2][:, 0, :], x_pairs[2][:, 1, :], x_rows[0][:], x_rows[1][:]]]
+        w2_first = keep.tile([P, PACK, H], F32, name="w2_first", align_bytes=64)
+        w2_last = [keep.tile([P, 2, H], F32, name=f"w2_last{u}", align_bytes=64) for u in range(2)]
         w1_codes = keep.tile([P, PASSES, 2 * N], U8, name="w1_codes", align_bytes=64)
         w3_codes = keep.tile([P, 2 * N], U8, name="w3_codes", align_bytes=64)
         w_scales = keep.tile([P, PASSES + 1, N], U8, name="w_scales", align_bytes=64)
@@ -47,10 +51,12 @@ def tile_picked_lora_relu_e_kernel(tc, xT, w1_words, w1_scales, w2, w3_words, w3
         nc.sync.dma_start(out=x_pairs[0][:], in_=x_view[0][:, 0:2, :])
         nc.sync.dma_start(offsets[:], offs)
         nc.sync.dma_start(out=x_pairs[1][:], in_=x_view[0][:, 2:4, :])
-        nc.sync.dma_start(out=w2_raw[0][:], in_=w2_view[0])
-        for j in range(PACK):
-            nc.sync.dma_start(out=x_rows[j][:], in_=x_view[1][:, j, :])
-        nc.sync.dma_start(out=w2_raw[1][:], in_=w2_view[1])
+        nc.sync.dma_start(out=x_pairs[2][:], in_=x_view[1][:, 0:2, :])
+        for j in range(2):
+            nc.sync.dma_start(out=x_rows[j][:], in_=x_view[1][:, 2 + j, :])
+        nc.sync.dma_start(out=w2_first[:], in_=w2_view[0])
+        for u in range(2):
+            nc.sync.dma_start(out=w2_last[u][:], in_=w2_view[1][:, 2 * u : 2 * u + 2, :])
         for q in range(4):
             nc.sync.dma_start(
                 out=w_scales[32 * q : 32 * q + 4, 0:PASSES, :].bitcast(I32),
@@ -65,10 +71,10 @@ def tile_picked_lora_relu_e_kernel(tc, xT, w1_words, w1_scales, w2, w3_words, w3
             )
 
         x_bf = [keep.tile([P, S, PACK], BF16, name=f"x_bf{z}", tag=f"x_bf{z}", align_bytes=64) for z in range(PASSES)]
-        x_codes = {}
+        x_codes = [keep.tile([P, S], U32, name=f"x_codes{z}", align_bytes=64) for z in range(PASSES)]
         x_scales = [keep.tile([P, S], U8, name=f"x_scales{z}", align_bytes=64) for z in range(PASSES)]
         w2_bf = [keep.tile([P, PACK, P, PACK], BF16, name=f"w2_bf{z}", tag=f"w2_bf{z}", align_bytes=64) for z in range(PASSES)]
-        w2_codes = {}
+        w2_codes = [keep.tile([P, PACK, P], U32, name=f"w2_codes{z}", align_bytes=64) for z in range(PASSES)]
         w2_scales = [keep.tile([P, PACK, P], U8, name=f"w2_scales{z}", align_bytes=64) for z in range(PASSES)]
         h_bank = [psum.tile([P, PACK, G], F32, name=f"h_bank{g}", tag=f"bank{g}") for g in range(GROUPS)]
         o_tile = [psum.tile([P, S], F32, name=f"o_bank{g}") for g in range(GROUPS)]
@@ -77,27 +83,23 @@ def tile_picked_lora_relu_e_kernel(tc, xT, w1_words, w1_scales, w2, w3_words, w3
         def gather(z, j, s0, s1):
             nc.vector.tensor_copy(out=x_bf[z][:, s0:s1, j], in_=windows[z][j].indirect(offsets[:, s0 // 16 : s1 // 16]))
 
-        def quantize_x(z, s0, s1, tag, step):
-            codes = keep.tile([P, s1 - s0], U32, name=f"x_codes{z}_{s0}", tag=tag, align_bytes=64)
-            for g in range(s0 // G, s1 // G):
-                x_codes[z, g] = codes[:, g * G - s0 : (g + 1) * G - s0]
-            x_codes[z, "all", s0] = codes[:]
-            for a in range(s0, s1, step):
-                nc.vector.quantize_mx(
-                    out=codes[:, a - s0 : a - s0 + step].bitcast(FP8X4),
-                    scales=x_scales[z][:, a : a + step],
-                    in_=x_bf[z][:, a : a + step].rearrange("p s j -> p (s j)"),
-                )
-
-        def w2_copy_views(z, m0, m1, t0, t1):
-            dst = w2_bf[z][:].rearrange("p t m j -> p m j t")[:, m0:m1, :, t0:t1]
-            src = w2_raw[z][:].rearrange("p j (m t) -> p m j t", t=PACK)[:, m0:m1, :, t0:t1]
-            return dst, src
-
-        def quantize_w2(z, t, tag):
-            w2_codes[z, t] = keep.tile([P, P], U32, name=f"w2_codes{z}{t}", tag=tag, align_bytes=64)
+        def quantize_x(z, s0, s1):
             nc.vector.quantize_mx(
-                out=w2_codes[z, t][:].bitcast(FP8X4),
+                out=x_codes[z][:, s0:s1].bitcast(FP8X4),
+                scales=x_scales[z][:, s0:s1],
+                in_=x_bf[z][:, s0:s1].rearrange("p s j -> p (s j)"),
+            )
+
+        def lay_out_w2(z, raw, j0, j1, m_vector):
+            for t0 in (0, 2):
+                dst = w2_bf[z][:].rearrange("p t m j -> p m j t")[:, :, j0:j1, t0 : t0 + 2]
+                src = raw[:].rearrange("p j (m t) -> p m j t", t=PACK)[:, :, :, t0 : t0 + 2]
+                nc.vector.tensor_copy(out=dst[:, 0:m_vector], in_=src[:, 0:m_vector])
+                nc.scalar.copy(out=dst[:, m_vector:P], in_=src[:, m_vector:P])
+
+        def quantize_w2(z, t):
+            nc.vector.quantize_mx(
+                out=w2_codes[z][:, t, :].bitcast(FP8X4),
                 scales=w2_scales[z][:, t, :],
                 in_=w2_bf[z][:, t].rearrange("p m j -> p (m j)"),
             )
@@ -106,9 +108,9 @@ def tile_picked_lora_relu_e_kernel(tc, xT, w1_words, w1_scales, w2, w3_words, w3
             cols = slice(g * G, (g + 1) * G)
             nc.tensor.matmul_mx(
                 out=h_bank[g][:, t, :],
-                lhsT=w2_codes[z, t][:].bitcast(FP8X4),
+                lhsT=w2_codes[z][:, t, :].bitcast(FP8X4),
                 lhsT_scale=w2_scales[z][:, t, :],
-                rhs=x_codes[z, g].bitcast(FP8X4),
+                rhs=x_codes[z][:, cols].bitcast(FP8X4),
                 rhs_scale=x_scales[z][:, cols],
                 start=start,
                 stop=stop,
@@ -116,48 +118,42 @@ def tile_picked_lora_relu_e_kernel(tc, xT, w1_words, w1_scales, w2, w3_words, w3
 
         for j in range(PACK):
             gather(0, j, 0, S)
-        quantize_x(0, 0, S, "x_codes0", S)
-        dst, src = w2_copy_views(0, 0, P, 0, PACK)
-        nc.scalar.copy(out=dst, in_=src)
         gather(1, 0, 0, S)
-        for t in range(1, PACK):
-            quantize_w2(0, t, f"w2_codes0{t}")
+        quantize_x(0, 0, S)
         gather(1, 1, 0, S)
         gather(1, 2, 0, S)
-        quantize_w2(0, 0, "x_rows2")
-        for g in range(GROUPS):
-            for t in range(PACK):
-                h_pass(0, g, t, start=(t == 0), stop=False)
         gather(1, 3, 0, S // 2)
         gather(1, 3, S // 2, S)
+        quantize_x(1, 0, S // 2)
+        quantize_x(1, S // 2, S)
 
-        def warm_up(s1):
+        for repeat in range(4):
             nc.tensor.matmul_mx(
-                out=o_tile[GROUPS - 1][:, 0:s1],
-                lhsT=w2_codes[0, 1][:].bitcast(FP8X4),
-                lhsT_scale=w2_scales[0][:, 1, :],
-                rhs=x_codes[1, "all", 0].bitcast(FP8X4),
-                rhs_scale=x_scales[1][:, 0:s1],
+                out=o_tile[GROUPS - 1][:, 0 : S // 2],
+                lhsT=x_codes[1][:, 0:P].bitcast(FP8X4),
+                lhsT_scale=x_scales[1][:, 0:P],
+                rhs=x_codes[1][:, 0 : S // 2].bitcast(FP8X4),
+                rhs_scale=x_scales[1][:, 0 : S // 2],
                 start=True,
                 stop=True,
             )
 
-        quantize_x(1, 0, S // 2, "x_codes1", S // 2)
-        for repeat in range(4):
-            warm_up(S // 2)
-
-        for t0 in (0, 2):
-            dst, src = w2_copy_views(1, 0, M_VECTOR, t0, t0 + 2)
-            nc.vector.tensor_copy(out=dst, in_=src)
-            dst, src = w2_copy_views(1, M_VECTOR, P, t0, t0 + 2)
-            nc.scalar.copy(out=dst, in_=src)
+        lay_out_w2(0, w2_first, 0, PACK, M_WHOLE)
         for t in range(PACK):
-            quantize_w2(1, t, f"w2_codes1{t}")
-        quantize_x(1, S // 2, S, "w2_raw1", G)
-        for pair in range(GROUPS // 2):
+            quantize_w2(0, t)
+        for t in range(PACK):
+            for g in range(GROUPS):
+                h_pass(0, g, t, start=(t == 0), stop=False)
+        lay_out_w2(1, w2_last[0], 0, 2, M_EARLY)
+        lay_out_w2(1, w2_last[1], 2, PACK, M_LATE)
+        for t in range(PACK):
+            quantize_w2(1, t)
+        for t in range(PACK):
+            for g in (0, 1):
+                h_pass(1, g, t, start=False, stop=(t == PACK - 1))
+        for g in (2, 3):
             for t in range(PACK):
-                for g in (2 * pair, 2 * pair + 1):
-                    h_pass(1, g, t, start=False, stop=(t == PACK - 1))
+                h_pass(1, g, t, start=False, stop=(t == PACK - 1))
 
         h_bf = [keep.tile([P, G, PACK], BF16, name=f"h_bf{g}", align_bytes=64) for g in range(GROUPS)]
         h_codes = [keep.tile([P, G], U32, name=f"h_codes{g}", align_bytes=64) for g in range(GROUPS)]
@@ -171,7 +167,7 @@ def tile_picked_lora_relu_e_kernel(tc, xT, w1_words, w1_scales, w2, w3_words, w3
             else:
                 nc.scalar.activation(out=h_bf[g][:, s0:s1], in_=src, func=RELU)
 
-        w1_plane = keep.tile([P, PASSES, N], U8, name="w1_plane", tag="x_bf1", align_bytes=64)
+        w1_plane = keep.tile([P, PASSES, N], U8, name="w1_plane", tag="w2_bf1", align_bytes=64)
         nc.gpsimd.tensor_copy(
             out=w1_plane[:].rearrange("p z c -> p (z c)").bitcast(I32),
             in_=w_scales[:, 0:PASSES, :].rearrange("p z c -> p (z c)").bitcast(I32),
@@ -184,7 +180,7 @@ def tile_picked_lora_relu_e_kernel(tc, xT, w1_words, w1_scales, w2, w3_words, w3
                     out=o_bank[g],
                     lhsT=w1_codes[:, z, :].bitcast(FP4X4),
                     lhsT_scale=w1_plane[:, z, :],
-                    rhs=x_codes[z, g].bitcast(FP8X4),
+                    rhs=x_codes[z][:, cols].bitcast(FP8X4),
                     rhs_scale=x_scales[z][:, cols],
                     start=(z == 0),
                     stop=False,
@@ -213,9 +209,9 @@ def tile_picked_lora_relu_e_kernel(tc, xT, w1_words, w1_scales, w2, w3_words, w3
         relu(1, True, 0, G)
         relu(2, False, 0, G)
         finish(0)
-        relu(3, True, 0, G // 2)
+        relu(3, True, 0, S_VECTOR)
         finish(1)
-        relu(3, False, G // 2, G)
+        relu(3, False, S_VECTOR, G)
         finish(2)
         finish(3)
         for g in range(GROUPS):

@@ -22,7 +22,7 @@ PASSES = K // K_PASS
 G = 128
 GROUPS = S // G
 M_WHOLE = 74
-M_EARLY = 48
+M_EARLY = 72
 S_VECTOR = 80
 M_LATE = 72
 
@@ -118,9 +118,11 @@ def tile_picked_lora_relu_e_kernel(tc, xT, w1_words, w1_scales, w2, w3_words, w3
 
         for j in range(PACK):
             gather(0, j, 0, S)
-        gather(1, 0, 0, S)
         quantize_x(0, 0, S)
-        gather(1, 1, 0, S)
+        picked = keep.tile([P, 2, S], F32, name="picked", align_bytes=64)
+        for j in range(2):
+            nc.vector.tensor_copy(out=picked[:, j, :], in_=windows[1][j].indirect(offsets[:]))
+        nc.scalar.copy(out=x_bf[1][:, :, 0:2], in_=picked[:].rearrange("p j s -> p s j"))
         gather(1, 2, 0, S)
         gather(1, 3, 0, S // 2)
         gather(1, 3, S // 2, S)

@@ -34,9 +34,12 @@ def tile_picked_lora_relu_e_kernel(tc, xT, w1_words, w1_scales, w2, w3_words, w3
         psum = ctx.enter_context(tc.psum_pool(name="psum", bufs=1))
 
         offsets = keep.tile([P, S // 16], U16, name="offsets")
-        x_pairs = [keep.tile([P, 2, T], F32, name=f"x_pair{u}", align_bytes=64) for u in range(3)]
-        x_rows = [keep.tile([P, T], F32, name=f"x_rows{j}", align_bytes=64) for j in range(2)]
-        windows = [[x_pairs[j // 2][:, j % 2, :] for j in range(PACK)], [x_pairs[2][:, 0, :], x_pairs[2][:, 1, :], x_rows[0][:], x_rows[1][:]]]
+        x_pairs = [keep.tile([P, 2, T], F32, name=f"x_pair{u}", align_bytes=64) for u in range(2)]
+        x_rows = [keep.tile([P, T], F32, name=f"x_rows{j}", align_bytes=64) for j in range(PACK)]
+        windows = [
+            [x_rows[0][:], x_rows[1][:], x_pairs[0][:, 0, :], x_pairs[0][:, 1, :]],
+            [x_pairs[1][:, 0, :], x_pairs[1][:, 1, :], x_rows[2][:], x_rows[3][:]],
+        ]
         w2_first = keep.tile([P, PACK, H], F32, name="w2_first", align_bytes=64)
         w2_last = [keep.tile([P, 2, H], F32, name=f"w2_last{u}", align_bytes=64) for u in range(2)]
         w1_codes = keep.tile([P, PASSES, 2 * N], U8, name="w1_codes", align_bytes=64)
@@ -48,12 +51,13 @@ def tile_picked_lora_relu_e_kernel(tc, xT, w1_words, w1_scales, w2, w3_words, w3
 
         nc.gpsimd.memset(w_scales[:].rearrange("p z c -> p (z c)").bitcast(I32), 0)
 
-        nc.sync.dma_start(out=x_pairs[0][:], in_=x_view[0][:, 0:2, :])
+        nc.scalar.dma_start(out=x_rows[0][:], in_=x_view[0][:, 0, :])
         nc.sync.dma_start(offsets[:], offs)
-        nc.sync.dma_start(out=x_pairs[1][:], in_=x_view[0][:, 2:4, :])
-        nc.sync.dma_start(out=x_pairs[2][:], in_=x_view[1][:, 0:2, :])
-        for j in range(2):
-            nc.sync.dma_start(out=x_rows[j][:], in_=x_view[1][:, 2 + j, :])
+        nc.sync.dma_start(out=x_rows[1][:], in_=x_view[0][:, 1, :])
+        nc.sync.dma_start(out=x_pairs[0][:], in_=x_view[0][:, 2:4, :])
+        nc.sync.dma_start(out=x_pairs[1][:], in_=x_view[1][:, 0:2, :])
+        for j in (2, 3):
+            nc.sync.dma_start(out=x_rows[j][:], in_=x_view[1][:, j, :])
         nc.sync.dma_start(out=w2_first[:], in_=w2_view[0])
         for u in range(2):
             nc.sync.dma_start(out=w2_last[u][:], in_=w2_view[1][:, 2 * u : 2 * u + 2, :])
@@ -71,7 +75,7 @@ def tile_picked_lora_relu_e_kernel(tc, xT, w1_words, w1_scales, w2, w3_words, w3
             )
 
         x_bf = [keep.tile([P, S, PACK], BF16, name=f"x_bf{z}", tag=f"x_bf{z}", align_bytes=64) for z in range(PASSES)]
-        x_codes = [keep.tile([P, S], U32, name=f"x_codes{z}", align_bytes=64) for z in range(PASSES)]
+        x_codes = {}
         x_scales = [keep.tile([P, S], U8, name=f"x_scales{z}", align_bytes=64) for z in range(PASSES)]
         w2_bf = [keep.tile([P, PACK, P, PACK], BF16, name=f"w2_bf{z}", tag=f"w2_bf{z}", align_bytes=64) for z in range(PASSES)]
         w2_codes = [keep.tile([P, PACK, P], U32, name=f"w2_codes{z}", align_bytes=64) for z in range(PASSES)]
@@ -83,12 +87,16 @@ def tile_picked_lora_relu_e_kernel(tc, xT, w1_words, w1_scales, w2, w3_words, w3
         def gather(z, j, s0, s1):
             nc.vector.tensor_copy(out=x_bf[z][:, s0:s1, j], in_=windows[z][j].indirect(offsets[:, s0 // 16 : s1 // 16]))
 
-        def quantize_x(z, s0, s1):
+        def quantize_x(z, s0, s1, tag):
+            codes = keep.tile([P, s1 - s0], U32, name=f"x_codes{z}_{s0}", tag=tag, align_bytes=64)
+            for g in range(s0 // G, s1 // G):
+                x_codes[z, g] = codes[:, g * G - s0 : (g + 1) * G - s0]
             nc.vector.quantize_mx(
-                out=x_codes[z][:, s0:s1].bitcast(FP8X4),
+                out=codes[:].bitcast(FP8X4),
                 scales=x_scales[z][:, s0:s1],
                 in_=x_bf[z][:, s0:s1].rearrange("p s j -> p (s j)"),
             )
+            return codes
 
         def lay_out_w2(z, raw, j0, j1, m_vector):
             for t0 in (0, 2):
@@ -110,7 +118,7 @@ def tile_picked_lora_relu_e_kernel(tc, xT, w1_words, w1_scales, w2, w3_words, w3
                 out=h_bank[g][:, t, :],
                 lhsT=w2_codes[z][:, t, :].bitcast(FP8X4),
                 lhsT_scale=w2_scales[z][:, t, :],
-                rhs=x_codes[z][:, cols].bitcast(FP8X4),
+                rhs=x_codes[z, g].bitcast(FP8X4),
                 rhs_scale=x_scales[z][:, cols],
                 start=start,
                 stop=stop,
@@ -118,7 +126,7 @@ def tile_picked_lora_relu_e_kernel(tc, xT, w1_words, w1_scales, w2, w3_words, w3
 
         for j in range(PACK):
             gather(0, j, 0, S)
-        quantize_x(0, 0, S)
+        quantize_x(0, 0, S, "x_codes0")
         picked = keep.tile([P, 2, S], F32, name="picked", align_bytes=64)
         for j in range(2):
             nc.vector.tensor_copy(out=picked[:, j, :], in_=windows[1][j].indirect(offsets[:]))
@@ -126,15 +134,15 @@ def tile_picked_lora_relu_e_kernel(tc, xT, w1_words, w1_scales, w2, w3_words, w3
         gather(1, 2, 0, S)
         gather(1, 3, 0, S // 2)
         gather(1, 3, S // 2, S)
-        quantize_x(1, 0, S // 2)
-        quantize_x(1, S // 2, S)
+        first_half = quantize_x(1, 0, S // 2, "x_codes1")
+        quantize_x(1, 2 * G, 3 * G, "x_codes2")
 
         for repeat in range(4):
             nc.tensor.matmul_mx(
                 out=o_tile[GROUPS - 1][:, 0 : S // 2],
-                lhsT=x_codes[1][:, 0:P].bitcast(FP8X4),
+                lhsT=first_half[:, 0:P].bitcast(FP8X4),
                 lhsT_scale=x_scales[1][:, 0:P],
-                rhs=x_codes[1][:, 0 : S // 2].bitcast(FP8X4),
+                rhs=first_half[:].bitcast(FP8X4),
                 rhs_scale=x_scales[1][:, 0 : S // 2],
                 start=True,
                 stop=True,
@@ -150,6 +158,7 @@ def tile_picked_lora_relu_e_kernel(tc, xT, w1_words, w1_scales, w2, w3_words, w3
         lay_out_w2(1, w2_last[1], 2, PACK, M_LATE)
         for t in range(PACK):
             quantize_w2(1, t)
+        quantize_x(1, 3 * G, S, "w2_bf1")
         for t in range(PACK):
             for g in (0, 1):
                 h_pass(1, g, t, start=False, stop=(t == PACK - 1))
@@ -169,7 +178,7 @@ def tile_picked_lora_relu_e_kernel(tc, xT, w1_words, w1_scales, w2, w3_words, w3
             else:
                 nc.scalar.activation(out=h_bf[g][:, s0:s1], in_=src, func=RELU)
 
-        w1_plane = keep.tile([P, PASSES, N], U8, name="w1_plane", tag="w2_bf1", align_bytes=64)
+        w1_plane = keep.tile([P, PASSES, N], U8, name="w1_plane", tag="x_bf1", align_bytes=64)
         nc.gpsimd.tensor_copy(
             out=w1_plane[:].rearrange("p z c -> p (z c)").bitcast(I32),
             in_=w_scales[:, 0:PASSES, :].rearrange("p z c -> p (z c)").bitcast(I32),
@@ -182,7 +191,7 @@ def tile_picked_lora_relu_e_kernel(tc, xT, w1_words, w1_scales, w2, w3_words, w3
                     out=o_bank[g],
                     lhsT=w1_codes[:, z, :].bitcast(FP4X4),
                     lhsT_scale=w1_plane[:, z, :],
-                    rhs=x_codes[z][:, cols].bitcast(FP8X4),
+                    rhs=x_codes[z, g].bitcast(FP8X4),
                     rhs_scale=x_scales[z][:, cols],
                     start=(z == 0),
                     stop=False,

@@ -21,10 +21,10 @@ K_PASS = P * PACK
 PASSES = K // K_PASS
 G = 128
 GROUPS = S // G
-M_WHOLE = 74
+M_WHOLE = 64
 M_EARLY = 72
 S_VECTOR = 80
-M_LATE = 72
+M_LATE = 80
 
 
 def tile_picked_lora_relu_e_kernel(tc, xT, w1_words, w1_scales, w2, w3_words, w3_scales, offs, out):
@@ -210,20 +210,21 @@ def tile_picked_lora_relu_e_kernel(tc, xT, w1_words, w1_scales, w2, w3_words, w3
             )
 
         def store(g):
-            nc.scalar.copy(out=result[g][:], in_=o_bank[g])
-            queue = nc.scalar if g == GROUPS - 1 else nc.sync
+            if g == 2:
+                nc.vector.tensor_copy(out=result[g][:], in_=o_bank[g])
+            else:
+                nc.scalar.copy(out=result[g][:], in_=o_bank[g])
+            queue = nc.scalar if g == 3 else nc.sync
             queue.dma_start(out=out[:, g * G : (g + 1) * G], in_=result[g][:])
 
         for g in range(GROUPS):
             w1_passes(g)
         relu(0, False, 0, G)
         relu(1, True, 0, G)
-        relu(2, False, 0, G)
-        finish(0)
-        relu(3, True, 0, S_VECTOR)
-        finish(1)
-        relu(3, False, S_VECTOR, G)
-        finish(2)
-        finish(3)
-        for g in range(GROUPS):
+        relu(2, True, 0, S_VECTOR)
+        relu(3, False, 0, G)
+        relu(2, False, S_VECTOR, G)
+        for g in (0, 1, 3, 2):
+            finish(g)
+        for g in (0, 1, 3, 2):
             store(g)

@@ -96,7 +96,6 @@ def tile_picked_lora_relu_e_kernel(tc, xT, w1_words, w1_scales, w2, w3_words, w3
                 scales=x_scales[z][:, s0:s1],
                 in_=x_bf[z][:, s0:s1].rearrange("p s j -> p (s j)"),
             )
-            return codes
 
         def lay_out_w2(z, raw, j0, j1, m_vector):
             for t0 in (0, 2):
@@ -134,19 +133,8 @@ def tile_picked_lora_relu_e_kernel(tc, xT, w1_words, w1_scales, w2, w3_words, w3
         gather(1, 2, 0, S)
         gather(1, 3, 0, S // 2)
         gather(1, 3, S // 2, S)
-        first_half = quantize_x(1, 0, S // 2, "x_codes1")
+        quantize_x(1, 0, S // 2, "x_codes1")
         quantize_x(1, 2 * G, 3 * G, "x_codes2")
-
-        for repeat in range(4):
-            nc.tensor.matmul_mx(
-                out=o_tile[GROUPS - 1][:, 0 : S // 2],
-                lhsT=first_half[:, 0:P].bitcast(FP8X4),
-                lhsT_scale=x_scales[1][:, 0:P],
-                rhs=first_half[:].bitcast(FP8X4),
-                rhs_scale=x_scales[1][:, 0 : S // 2],
-                start=True,
-                stop=True,
-            )
 
         lay_out_w2(0, w2_first, 0, PACK, M_WHOLE)
         for t in range(PACK):

@@ -21,6 +21,7 @@ K_PASS = P * PACK
 PASSES = K // K_PASS
 G = 128
 GROUPS = S // G
+WARM_M = 64
 M_WHOLE = 64
 M_EARLY = 72
 S_VECTOR = 80
@@ -96,6 +97,7 @@ def tile_picked_lora_relu_e_kernel(tc, xT, w1_words, w1_scales, w2, w3_words, w3
                 scales=x_scales[z][:, s0:s1],
                 in_=x_bf[z][:, s0:s1].rearrange("p s j -> p (s j)"),
             )
+            return codes
 
         def lay_out_w2(z, raw, j0, j1, m_vector):
             for t0 in (0, 2):
@@ -125,7 +127,7 @@ def tile_picked_lora_relu_e_kernel(tc, xT, w1_words, w1_scales, w2, w3_words, w3
 
         for j in range(PACK):
             gather(0, j, 0, S)
-        quantize_x(0, 0, S, "x_codes0")
+        first_pass = quantize_x(0, 0, S, "x_codes0")
         picked = keep.tile([P, 2, S], F32, name="picked", align_bytes=64)
         for j in range(2):
             nc.vector.tensor_copy(out=picked[:, j, :], in_=windows[1][j].indirect(offsets[:]))
@@ -133,8 +135,19 @@ def tile_picked_lora_relu_e_kernel(tc, xT, w1_words, w1_scales, w2, w3_words, w3
         gather(1, 2, 0, S)
         gather(1, 3, 0, S // 2)
         gather(1, 3, S // 2, S)
-        quantize_x(1, 0, S // 2, "x_codes1")
+        first_half = quantize_x(1, 0, S // 2, "x_codes1")
         quantize_x(1, 2 * G, 3 * G, "x_codes2")
+
+        for repeat in range(2):
+            nc.tensor.matmul_mx(
+                out=o_tile[GROUPS - 1][0:WARM_M, :],
+                lhsT=first_half[:, 0:WARM_M].bitcast(FP8X4),
+                lhsT_scale=x_scales[1][:, 0:WARM_M],
+                rhs=first_pass[:].bitcast(FP8X4),
+                rhs_scale=x_scales[0][:],
+                start=True,
+                stop=True,
+            )
 
         lay_out_w2(0, w2_first, 0, PACK, M_WHOLE)
         for t in range(PACK):

@@ -21,6 +21,7 @@ K_PASS = P * PACK
 PASSES = K // K_PASS
 G = 128
 GROUPS = S // G
+BURST = 256
 WARM_M = 64
 M_WHOLE = 64
 M_EARLY = 72
@@ -35,14 +36,14 @@ def tile_picked_lora_relu_e_kernel(tc, xT, w1_words, w1_scales, w2, w3_words, w3
         psum = ctx.enter_context(tc.psum_pool(name="psum", bufs=1))
 
         offsets = keep.tile([P, S // 16], U16, name="offsets")
-        x_pairs = [keep.tile([P, 2, T], F32, name=f"x_pair{u}", align_bytes=64) for u in range(2)]
-        x_rows = [keep.tile([P, T], F32, name=f"x_rows{j}", align_bytes=64) for j in range(PACK)]
+        x_pairs = [keep.tile([P, 2, T], F32, name=f"x_pair{u}", align_bytes=BURST) for u in range(2)]
+        x_rows = [keep.tile([P, T], F32, name=f"x_rows{j}", align_bytes=BURST) for j in range(PACK)]
         windows = [
             [x_rows[0][:], x_rows[1][:], x_pairs[0][:, 0, :], x_pairs[0][:, 1, :]],
             [x_pairs[1][:, 0, :], x_pairs[1][:, 1, :], x_rows[2][:], x_rows[3][:]],
         ]
-        w2_first = keep.tile([P, PACK, H], F32, name="w2_first", align_bytes=64)
-        w2_last = [keep.tile([P, 2, H], F32, name=f"w2_last{u}", align_bytes=64) for u in range(2)]
+        w2_first = keep.tile([P, PACK, H], F32, name="w2_first", align_bytes=BURST)
+        w2_last = [keep.tile([P, 2, H], F32, name=f"w2_last{u}", align_bytes=BURST) for u in range(2)]
         w1_codes = keep.tile([P, PASSES, 2 * N], U8, name="w1_codes", align_bytes=64)
         w3_codes = keep.tile([P, 2 * N], U8, name="w3_codes", align_bytes=64)
         w_scales = keep.tile([P, PASSES + 1, N], U8, name="w_scales", align_bytes=64)
@@ -170,7 +171,7 @@ def tile_picked_lora_relu_e_kernel(tc, xT, w1_words, w1_scales, w2, w3_words, w3
         h_bf = [keep.tile([P, G, PACK], BF16, name=f"h_bf{g}", align_bytes=64) for g in range(GROUPS)]
         h_codes = [keep.tile([P, G], U32, name=f"h_codes{g}", align_bytes=64) for g in range(GROUPS)]
         h_scales = [keep.tile([P, G], U8, name=f"h_scales{g}", align_bytes=64) for g in range(GROUPS)]
-        result = [keep.tile([P, G], F32, name=f"result{g}") for g in range(GROUPS)]
+        result = [keep.tile([P, G], F32, name=f"result{g}", align_bytes=BURST) for g in range(GROUPS)]
 
         def relu(g, on_vector, s0, s1):
             src = h_bank[g][:].rearrange("p t s -> p s t")[:, s0:s1]

@@ -23,10 +23,12 @@ G = 128
 GROUPS = S // G
 BURST = 256
 WARM_M = 64
-M_WHOLE = 64
-M_EARLY = 72
+M_WHOLE = 80
+M_HALF = 42
+M_AHEAD = (26, 40)
+M_BEHIND = 84
 S_VECTOR = 80
-M_LATE = 80
+W2_END = H // 2
 
 
 def tile_picked_lora_relu_e_kernel(tc, xT, w1_words, w1_scales, w2, w3_words, w3_scales, offs, out):
@@ -43,13 +45,13 @@ def tile_picked_lora_relu_e_kernel(tc, xT, w1_words, w1_scales, w2, w3_words, w3
             [x_pairs[1][:, 0, :], x_pairs[1][:, 1, :], x_rows[2][:], x_rows[3][:]],
         ]
         w2_first = keep.tile([P, PACK, H], F32, name="w2_first", align_bytes=BURST)
-        w2_last = [keep.tile([P, 2, H], F32, name=f"w2_last{u}", align_bytes=BURST) for u in range(2)]
+        w2_last = keep.tile([P, PACK, H], F32, name="w2_last", align_bytes=BURST)
         w1_codes = keep.tile([P, PASSES, 2 * N], U8, name="w1_codes", align_bytes=64)
         w3_codes = keep.tile([P, 2 * N], U8, name="w3_codes", align_bytes=64)
         w_scales = keep.tile([P, PASSES + 1, N], U8, name="w_scales", align_bytes=64)
 
         x_view = xT.rearrange("(z p j) t -> z p j t", z=PASSES, j=PACK)
-        w2_view = w2.rearrange("(z p j) c -> z p j c", z=PASSES, j=PACK)
+        w2_view = w2.rearrange("(z p j) c -> z p (j c)", z=PASSES, j=PACK)
 
         nc.gpsimd.memset(w_scales[:].rearrange("p z c -> p (z c)").bitcast(I32), 0)
 
@@ -60,9 +62,11 @@ def tile_picked_lora_relu_e_kernel(tc, xT, w1_words, w1_scales, w2, w3_words, w3
         nc.sync.dma_start(out=x_pairs[1][:], in_=x_view[1][:, 0:2, :])
         for j in (2, 3):
             nc.sync.dma_start(out=x_rows[j][:], in_=x_view[1][:, j, :])
-        nc.sync.dma_start(out=w2_first[:], in_=w2_view[0])
-        for u in range(2):
-            nc.sync.dma_start(out=w2_last[u][:], in_=w2_view[1][:, 2 * u : 2 * u + 2, :])
+        nc.sync.dma_start(out=w2_first[:].rearrange("p j c -> p (j c)"), in_=w2_view[0])
+        cut = PACK * H - W2_END
+        w2_last_flat = w2_last[:].rearrange("p j c -> p (j c)")
+        nc.sync.dma_start(out=w2_last_flat[:, 0:cut], in_=w2_view[1][:, 0:cut])
+        nc.sync.dma_start(out=w2_last_flat[:, cut:], in_=w2_view[1][:, cut:])
         for q in range(4):
             nc.sync.dma_start(
                 out=w_scales[32 * q : 32 * q + 4, 0:PASSES, :].bitcast(I32),
@@ -100,12 +104,11 @@ def tile_picked_lora_relu_e_kernel(tc, xT, w1_words, w1_scales, w2, w3_words, w3
             )
             return codes
 
-        def lay_out_w2(z, raw, j0, j1, m_vector):
-            for t0 in (0, 2):
-                dst = w2_bf[z][:].rearrange("p t m j -> p m j t")[:, :, j0:j1, t0 : t0 + 2]
-                src = raw[:].rearrange("p j (m t) -> p m j t", t=PACK)[:, :, :, t0 : t0 + 2]
-                nc.vector.tensor_copy(out=dst[:, 0:m_vector], in_=src[:, 0:m_vector])
-                nc.scalar.copy(out=dst[:, m_vector:P], in_=src[:, m_vector:P])
+        def lay_out_w2(z, raw, t0, on_vector, on_scalar):
+            dst = w2_bf[z][:].rearrange("p t m j -> p m j t")[:, :, :, t0 : t0 + 2]
+            src = raw[:].rearrange("p j (m t) -> p m j t", t=PACK)[:, :, :, t0 : t0 + 2]
+            nc.vector.tensor_copy(out=dst[:, on_vector], in_=src[:, on_vector])
+            nc.scalar.copy(out=dst[:, on_scalar], in_=src[:, on_scalar])
 
         def quantize_w2(z, t):
             nc.vector.quantize_mx(
@@ -150,14 +153,18 @@ def tile_picked_lora_relu_e_kernel(tc, xT, w1_words, w1_scales, w2, w3_words, w3
                 stop=True,
             )
 
-        lay_out_w2(0, w2_first, 0, PACK, M_WHOLE)
+        for t0 in (0, 2):
+            lay_out_w2(0, w2_first, t0, slice(0, M_WHOLE), slice(M_WHOLE, P))
         for t in range(PACK):
             quantize_w2(0, t)
         for t in range(PACK):
             for g in range(GROUPS):
                 h_pass(0, g, t, start=(t == 0), stop=False)
-        lay_out_w2(1, w2_last[0], 0, 2, M_EARLY)
-        lay_out_w2(1, w2_last[1], 2, PACK, M_LATE)
+        half = P // 2
+        lay_out_w2(1, w2_last, 0, slice(0, M_HALF), slice(M_HALF, half))
+        lay_out_w2(1, w2_last, 2, slice(0, M_AHEAD[0]), slice(M_AHEAD[0], M_AHEAD[1]))
+        lay_out_w2(1, w2_last, 0, slice(half, half + M_HALF), slice(half + M_HALF, P))
+        lay_out_w2(1, w2_last, 2, slice(M_BEHIND, P), slice(M_AHEAD[1], M_BEHIND))
         for t in range(PACK):
             quantize_w2(1, t)
         quantize_x(1, 3 * G, S, "w2_bf1")

@@ -25,9 +25,10 @@ BURST = 256
 WARM_M = 64
 M_WHOLE = 80
 M_HALF = 42
+M_FIRST = 34
 M_AHEAD = (26, 40)
-M_BEHIND = 84
-S_VECTOR = 80
+M_BEHIND = 78
+S_VECTOR = 72
 W2_END = H // 2
 
 
@@ -163,7 +164,7 @@ def tile_picked_lora_relu_e_kernel(tc, xT, w1_words, w1_scales, w2, w3_words, w3
         half = P // 2
         lay_out_w2(1, w2_last, 0, slice(0, M_HALF), slice(M_HALF, half))
         lay_out_w2(1, w2_last, 2, slice(0, M_AHEAD[0]), slice(M_AHEAD[0], M_AHEAD[1]))
-        lay_out_w2(1, w2_last, 0, slice(half, half + M_HALF), slice(half + M_HALF, P))
+        lay_out_w2(1, w2_last, 0, slice(half, half + M_FIRST), slice(half + M_FIRST, P))
         lay_out_w2(1, w2_last, 2, slice(M_BEHIND, P), slice(M_AHEAD[1], M_BEHIND))
         for t in range(PACK):
             quantize_w2(1, t)
@@ -219,21 +220,21 @@ def tile_picked_lora_relu_e_kernel(tc, xT, w1_words, w1_scales, w2, w3_words, w3
             )
 
         def store(g):
-            if g == 2:
+            if g == 3:
                 nc.vector.tensor_copy(out=result[g][:], in_=o_bank[g])
             else:
                 nc.scalar.copy(out=result[g][:], in_=o_bank[g])
-            queue = nc.scalar if g == 3 else nc.sync
+            queue = nc.scalar if g == 2 else nc.sync
             queue.dma_start(out=out[:, g * G : (g + 1) * G], in_=result[g][:])
 
         for g in range(GROUPS):
             w1_passes(g)
         relu(0, False, 0, G)
         relu(1, True, 0, G)
-        relu(2, True, 0, S_VECTOR)
-        relu(3, False, 0, G)
-        relu(2, False, S_VECTOR, G)
-        for g in (0, 1, 3, 2):
+        relu(2, False, 0, G)
+        relu(3, True, 0, S_VECTOR)
+        relu(3, False, S_VECTOR, G)
+        for g in range(GROUPS):
             finish(g)
-        for g in (0, 1, 3, 2):
+        for g in range(GROUPS):
             store(g)

@@ -28,7 +28,6 @@ M_HALF = 42
 M_FIRST = 34
 M_AHEAD = (26, 40)
 M_BEHIND = 78
-S_VECTOR = 72
 W2_END = H // 2
 
 
@@ -229,11 +228,8 @@ def tile_picked_lora_relu_e_kernel(tc, xT, w1_words, w1_scales, w2, w3_words, w3
 
         for g in range(GROUPS):
             w1_passes(g)
-        relu(0, False, 0, G)
-        relu(1, True, 0, G)
-        relu(2, False, 0, G)
-        relu(3, True, 0, S_VECTOR)
-        relu(3, False, S_VECTOR, G)
+        for g in range(GROUPS):
+            relu(g, g % 2 == 0, 0, G)
         for g in range(GROUPS):
             finish(g)
         for g in range(GROUPS):

@@ -187,19 +187,13 @@ def tile_picked_lora_relu_e_kernel(tc, xT, w1_words, w1_scales, w2, w3_words, w3
             else:
                 nc.scalar.activation(out=h_bf[g][:, s0:s1], in_=src, func=RELU)
 
-        w1_plane = keep.tile([P, PASSES, N], U8, name="w1_plane", tag="x_bf1", align_bytes=64)
-        nc.gpsimd.tensor_copy(
-            out=w1_plane[:].rearrange("p z c -> p (z c)").bitcast(I32),
-            in_=w_scales[:, 0:PASSES, :].rearrange("p z c -> p (z c)").bitcast(I32),
-        )
-
         def w1_passes(g):
             cols = slice(g * G, (g + 1) * G)
             for z in range(PASSES):
                 nc.tensor.matmul_mx(
                     out=o_bank[g],
                     lhsT=w1_codes[:, z, :].bitcast(FP4X4),
-                    lhsT_scale=w1_plane[:, z, :],
+                    lhsT_scale=w_scales[:, z, :],
                     rhs=x_codes[z, g].bitcast(FP8X4),
                     rhs_scale=x_scales[z][:, cols],
                     start=(z == 0),

from contextlib import ExitStack

import concourse.mybir as mybir

K, T, S, H, N = 1024, 2048, 512, 512, 128
FLOPS = 2 * S * (K * H + K * N + H * N)

F32 = mybir.dt.float32
BF16 = mybir.dt.bfloat16
I32 = mybir.dt.int32
U32 = mybir.dt.uint32
U16 = mybir.dt.uint16
U8 = mybir.dt.uint8
FP8X4 = mybir.dt.float8_e4m3fn_x4
FP4X4 = mybir.dt.float4_e2m1fn_x4
RELU = mybir.ActivationFunctionType.Relu

P = 128
PACK = 4
K_PASS = P * PACK
PASSES = K // K_PASS
G = 128
GROUPS = S // G
BURST = 256
WARM_M = 64
M_WHOLE = 80
M_HALF = 42
M_FIRST = 34
M_AHEAD = (26, 40)
M_BEHIND = 78
W2_END = H // 2


def tile_picked_lora_relu_e_kernel(tc, xT, w1_words, w1_scales, w2, w3_words, w3_scales, offs, out):
    nc = tc.nc
    with ExitStack() as ctx:
        keep = ctx.enter_context(tc.tile_pool(name="keep", bufs=1))
        psum = ctx.enter_context(tc.psum_pool(name="psum", bufs=1))

        offsets = keep.tile([P, S // 16], U16, name="offsets")
        x_pairs = [keep.tile([P, 2, T], F32, name=f"x_pair{u}", align_bytes=BURST) for u in range(2)]
        x_rows = [keep.tile([P, T], F32, name=f"x_rows{j}", align_bytes=BURST) for j in range(PACK)]
        windows = [
            [x_rows[0][:], x_rows[1][:], x_pairs[0][:, 0, :], x_pairs[0][:, 1, :]],
            [x_pairs[1][:, 0, :], x_pairs[1][:, 1, :], x_rows[2][:], x_rows[3][:]],
        ]
        w2_first = keep.tile([P, PACK, H], F32, name="w2_first", align_bytes=BURST)
        w2_last = keep.tile([P, PACK, H], F32, name="w2_last", align_bytes=BURST)
        w1_codes = keep.tile([P, PASSES, 2 * N], U8, name="w1_codes", align_bytes=64)
        w3_codes = keep.tile([P, 2 * N], U8, name="w3_codes", align_bytes=64)
        w_scales = keep.tile([P, PASSES + 1, N], U8, name="w_scales", align_bytes=64)

        x_view = xT.rearrange("(z p j) t -> z p j t", z=PASSES, j=PACK)
        w2_view = w2.rearrange("(z p j) c -> z p (j c)", z=PASSES, j=PACK)

        nc.gpsimd.memset(w_scales[:].rearrange("p z c -> p (z c)").bitcast(I32), 0)

        nc.scalar.dma_start(out=x_rows[0][:], in_=x_view[0][:, 0, :])
        nc.sync.dma_start(offsets[:], offs)
        nc.sync.dma_start(out=x_rows[1][:], in_=x_view[0][:, 1, :])
        nc.sync.dma_start(out=x_pairs[0][:], in_=x_view[0][:, 2:4, :])
        nc.sync.dma_start(out=x_pairs[1][:], in_=x_view[1][:, 0:2, :])
        for j in (2, 3):
            nc.sync.dma_start(out=x_rows[j][:], in_=x_view[1][:, j, :])
        nc.sync.dma_start(out=w2_first[:].rearrange("p j c -> p (j c)"), in_=w2_view[0])
        cut = PACK * H - W2_END
        w2_last_flat = w2_last[:].rearrange("p j c -> p (j c)")
        nc.sync.dma_start(out=w2_last_flat[:, 0:cut], in_=w2_view[1][:, 0:cut])
        nc.sync.dma_start(out=w2_last_flat[:, cut:], in_=w2_view[1][:, cut:])
        for q in range(4):
            nc.sync.dma_start(
                out=w_scales[32 * q : 32 * q + 4, 0:PASSES, :].bitcast(I32),
                in_=w1_scales[:, 4 * q : 4 * q + 4, :].rearrange("z r c -> r z c").bitcast(I32),
            )
        nc.sync.dma_start(out=w1_codes[:].bitcast(I32), in_=w1_words.rearrange("z p b -> p z b").bitcast(I32))
        nc.sync.dma_start(out=w3_codes[:].bitcast(I32), in_=w3_words[0].bitcast(I32))
        for q in range(4):
            nc.sync.dma_start(
                out=w_scales[32 * q : 32 * q + 4, PASSES, :].bitcast(I32),
                in_=w3_scales[0, 4 * q : 4 * q + 4, :].bitcast(I32),
            )

        x_bf = [keep.tile([P, S, PACK], BF16, name=f"x_bf{z}", tag=f"x_bf{z}", align_bytes=64) for z in range(PASSES)]
        x_codes = {}
        x_scales = [keep.tile([P, S], U8, name=f"x_scales{z}", align_bytes=64) for z in range(PASSES)]
        w2_bf = [keep.tile([P, PACK, P, PACK], BF16, name=f"w2_bf{z}", tag=f"w2_bf{z}", align_bytes=64) for z in range(PASSES)]
        w2_codes = [keep.tile([P, PACK, P], U32, name=f"w2_codes{z}", align_bytes=64) for z in range(PASSES)]
        w2_scales = [keep.tile([P, PACK, P], U8, name=f"w2_scales{z}", align_bytes=64) for z in range(PASSES)]
        h_bank = [psum.tile([P, PACK, G], F32, name=f"h_bank{g}", tag=f"bank{g}") for g in range(GROUPS)]
        o_tile = [psum.tile([P, S], F32, name=f"o_bank{g}") for g in range(GROUPS)]
        o_bank = [o_tile[g][:, 0:G] for g in range(GROUPS)]

        def gather(z, j, s0, s1):
            nc.vector.tensor_copy(out=x_bf[z][:, s0:s1, j], in_=windows[z][j].indirect(offsets[:, s0 // 16 : s1 // 16]))

        def quantize_x(z, s0, s1, tag):
            codes = keep.tile([P, s1 - s0], U32, name=f"x_codes{z}_{s0}", tag=tag, align_bytes=64)
            for g in range(s0 // G, s1 // G):
                x_codes[z, g] = codes[:, g * G - s0 : (g + 1) * G - s0]
            nc.vector.quantize_mx(
                out=codes[:].bitcast(FP8X4),
                scales=x_scales[z][:, s0:s1],
                in_=x_bf[z][:, s0:s1].rearrange("p s j -> p (s j)"),
            )
            return codes

        def lay_out_w2(z, raw, t0, on_vector, on_scalar):
            dst = w2_bf[z][:].rearrange("p t m j -> p m j t")[:, :, :, t0 : t0 + 2]
            src = raw[:].rearrange("p j (m t) -> p m j t", t=PACK)[:, :, :, t0 : t0 + 2]
            nc.vector.tensor_copy(out=dst[:, on_vector], in_=src[:, on_vector])
            nc.scalar.copy(out=dst[:, on_scalar], in_=src[:, on_scalar])

        def quantize_w2(z, t):
            nc.vector.quantize_mx(
                out=w2_codes[z][:, t, :].bitcast(FP8X4),
                scales=w2_scales[z][:, t, :],
                in_=w2_bf[z][:, t].rearrange("p m j -> p (m j)"),
            )

        def h_pass(z, g, t, start, stop):
            cols = slice(g * G, (g + 1) * G)
            nc.tensor.matmul_mx(
                out=h_bank[g][:, t, :],
                lhsT=w2_codes[z][:, t, :].bitcast(FP8X4),
                lhsT_scale=w2_scales[z][:, t, :],
                rhs=x_codes[z, g].bitcast(FP8X4),
                rhs_scale=x_scales[z][:, cols],
                start=start,
                stop=stop,
            )

        for j in range(PACK):
            gather(0, j, 0, S)
        first_pass = quantize_x(0, 0, S, "x_codes0")
        picked = keep.tile([P, 2, S], F32, name="picked", align_bytes=64)
        for j in range(2):
            nc.vector.tensor_copy(out=picked[:, j, :], in_=windows[1][j].indirect(offsets[:]))
        nc.scalar.copy(out=x_bf[1][:, :, 0:2], in_=picked[:].rearrange("p j s -> p s j"))
        gather(1, 2, 0, S)
        gather(1, 3, 0, S // 2)
        gather(1, 3, S // 2, S)
        first_half = quantize_x(1, 0, S // 2, "x_codes1")
        quantize_x(1, 2 * G, 3 * G, "x_codes2")

        for repeat in range(2):
            nc.tensor.matmul_mx(
                out=o_tile[GROUPS - 1][0:WARM_M, :],
                lhsT=first_half[:, 0:WARM_M].bitcast(FP8X4),
                lhsT_scale=x_scales[1][:, 0:WARM_M],
                rhs=first_pass[:].bitcast(FP8X4),
                rhs_scale=x_scales[0][:],
                start=True,
                stop=True,
            )

        for t0 in (0, 2):
            lay_out_w2(0, w2_first, t0, slice(0, M_WHOLE), slice(M_WHOLE, P))
        for t in range(PACK):
            quantize_w2(0, t)
        for t in range(PACK):
            for g in range(GROUPS):
                h_pass(0, g, t, start=(t == 0), stop=False)
        half = P // 2
        lay_out_w2(1, w2_last, 0, slice(0, M_HALF), slice(M_HALF, half))
        lay_out_w2(1, w2_last, 2, slice(0, M_AHEAD[0]), slice(M_AHEAD[0], M_AHEAD[1]))
        lay_out_w2(1, w2_last, 0, slice(half, half + M_FIRST), slice(half + M_FIRST, P))
        lay_out_w2(1, w2_last, 2, slice(M_BEHIND, P), slice(M_AHEAD[1], M_BEHIND))
        for t in range(PACK):
            quantize_w2(1, t)
        quantize_x(1, 3 * G, S, "w2_bf1")
        for t in range(PACK):
            for g in (0, 1):
                h_pass(1, g, t, start=False, stop=(t == PACK - 1))
        for g in (2, 3):
            for t in range(PACK):
                h_pass(1, g, t, start=False, stop=(t == PACK - 1))

        h_bf = [keep.tile([P, G, PACK], BF16, name=f"h_bf{g}", align_bytes=64) for g in range(GROUPS)]
        h_codes = [keep.tile([P, G], U32, name=f"h_codes{g}", align_bytes=64) for g in range(GROUPS)]
        h_scales = [keep.tile([P, G], U8, name=f"h_scales{g}", align_bytes=64) for g in range(GROUPS)]
        result = [keep.tile([P, G], F32, name=f"result{g}", align_bytes=BURST) for g in range(GROUPS)]

        def relu(g, on_vector, s0, s1):
            src = h_bank[g][:].rearrange("p t s -> p s t")[:, s0:s1]
            if on_vector:
                nc.vector.tensor_scalar_max(out=h_bf[g][:, s0:s1], in0=src, scalar1=0.0)
            else:
                nc.scalar.activation(out=h_bf[g][:, s0:s1], in_=src, func=RELU)

        def w1_passes(g):
            cols = slice(g * G, (g + 1) * G)
            for z in range(PASSES):
                nc.tensor.matmul_mx(
                    out=o_bank[g],
                    lhsT=w1_codes[:, z, :].bitcast(FP4X4),
                    lhsT_scale=w_scales[:, z, :],
                    rhs=x_codes[z, g].bitcast(FP8X4),
                    rhs_scale=x_scales[z][:, cols],
                    start=(z == 0),
                    stop=False,
                )

        def finish(g):
            nc.vector.quantize_mx(out=h_codes[g][:].bitcast(FP8X4), scales=h_scales[g][:], in_=h_bf[g][:].rearrange("p s t -> p (s t)"))
            nc.tensor.matmul_mx(
                out=o_bank[g],
                lhsT=w3_codes[:].bitcast(FP4X4),
                lhsT_scale=w_scales[:, PASSES, :],
                rhs=h_codes[g][:].bitcast(FP8X4),
                rhs_scale=h_scales[g][:],
                start=False,
                stop=True,
            )

        def store(g):
            if g == 3:
                nc.vector.tensor_copy(out=result[g][:], in_=o_bank[g])
            else:
                nc.scalar.copy(out=result[g][:], in_=o_bank[g])
            queue = nc.scalar if g == 2 else nc.sync
            queue.dma_start(out=out[:, g * G : (g + 1) * G], in_=result[g][:])

        for g in range(GROUPS):
            w1_passes(g)
        for g in range(GROUPS):
            relu(g, g % 2 == 0, 0, G)
        for g in range(GROUPS):
            finish(g)
        for g in range(GROUPS):
            store(g)
